import numpy as np
import ml_dtypes


def mxq(x, axis, fmt="e4m3"):
    dtype, down = {"e4m3": (ml_dtypes.float8_e4m3fn, 7), "e5m2": (ml_dtypes.float8_e5m2, 14)}[fmt]
    v = np.moveaxis(np.asarray(x, np.float32).astype(ml_dtypes.bfloat16).astype(np.float64), axis, -1)
    blocks = v.reshape(v.shape[:-1] + (-1, 32))
    amax = np.abs(blocks).max(-1, keepdims=True)
    byte = np.maximum(np.where(amax > 0, np.frexp(amax)[1] - 1 + 127, 0) - down, 1)
    scale = np.exp2(byte - 127.0)
    codes = (blocks / scale).astype(np.float32).astype(dtype).astype(np.float64)
    return np.moveaxis((codes * scale).reshape(v.shape), -1, axis)


WIDE = False


def mx_kscale(k):
    if not WIDE:
        return np.ones(k)
    levels = np.array([10, -10, 5, -5, 0])
    if k % 512:
        return np.exp2(np.random.permutation(np.resize(levels, k // 32))).repeat(32)
    a = np.empty((k // 512, 16))
    for p in range(k // 512):
        a[p, :8] = np.random.permutation(np.resize(levels, 8))
        for g in range(8):
            far = levels[np.abs(levels - a[p, g]) >= 10]
            a[p, g + 8] = far[np.random.randint(len(far))]
    return np.exp2(a.ravel()).repeat(32)


BF16 = ml_dtypes.bfloat16


def bf(x):
    return np.asarray(x, np.float32).astype(BF16)


def f64(x):
    return np.asarray(x).astype(np.float64)


B, S, D, P = 2, 2048, 256, 512
S1 = S // 2


def gelu_tanh(v):
    return 0.5 * v * (1.0 + np.tanh(np.sqrt(2.0 / np.pi) * (v + 0.044715 * (v * v * v))))


def pool_pairs(x):
    b, s, d = x.shape
    pairs = x.reshape(b, s // 2, 2, d)
    return (pairs[:, :, 0, :] + pairs[:, :, 1, :]) / 2.0


def draw0():
    s, t = mx_kscale(S), mx_kscale(S1)
    return {
        "x": bf(np.random.standard_normal((B, S, D))),
        "g0": bf((1.0 + 0.1 * np.random.standard_normal(S)) * s),
        "w01": bf(np.random.standard_normal((S1, S)) / np.sqrt(S) / s[None, :]),
        "g1": bf((1.0 + 0.1 * np.random.standard_normal(S1)) * t),
        "f0": bf(np.random.standard_normal((P, S)) / np.sqrt(S) / s[None, :]),
        "f1": bf(np.random.standard_normal((P, S1)) / np.sqrt(S1) / t[None, :]),
        "ens": bf(np.random.standard_normal(P)),
    }


def core(x, g0, w01, g1, f0, f1, ens):
    xf = f64(x)
    u = mxq(f64(g0)[None, :, None] * xf, 1, "e4m3")
    x1 = pool_pairs(xf)
    m = mxq(f64(w01), 1, "e4m3") @ u
    y1 = f64(g1)[None, :, None] * (x1 + gelu_tanh(m))
    h0 = mxq(f64(f0), 1, "e4m3") @ u
    h1 = mxq(f64(f1), 1, "e4m3") @ mxq(y1, 1, "e4m3")
    a = (1.0 / (1.0 + np.exp(-f64(ens))))[None, :, None]
    return a * h0 + (1.0 - a) * h1


def e4m3fn_bytes(y):
    return np.clip(np.asarray(y, np.float64), -448.0, 448.0).astype(np.float32).astype(ml_dtypes.float8_e4m3fn).view(np.uint8)


def e4m3fn_values(b):
    return np.asarray(b, np.uint8).view(ml_dtypes.float8_e4m3fn).astype(np.float64)


def setup_inputs():
    d = draw0()
    x0 = np.asarray(d['w01']).astype(np.float64)
    s = (np.max(np.abs(x0), axis=(0,), keepdims=True) / 448.0).astype(np.float32)
    out = {}
    for k, v in d.items():
        if k == 'w01':
            out['w01_bytes'] = e4m3fn_bytes(x0 / s.astype(np.float64))
            out['w01_scale'] = s
        else:
            out[k] = v
    return out


def reference(x, g0, w01_bytes, w01_scale, g1, f0, f1, ens):
    return core(x, g0, e4m3fn_values(w01_bytes) * w01_scale.astype(np.float64), g1, f0, f1, ens)

@@ -1,0 +1,470 @@
+from contextlib import ExitStack
+
+import concourse.mybir as mybir
+from concourse.masks import make_identity
+
+F32 = mybir.dt.float32
+BF16 = mybir.dt.bfloat16
+U32 = mybir.dt.uint32
+U8 = mybir.dt.uint8
+FP8 = mybir.dt.float8_e4m3fn
+FP8X4 = mybir.dt.float8_e4m3fn_x4
+ACT = mybir.ActivationFunctionType
+ALU = mybir.AluOpType
+
+P = 128
+B, S, D, HZ = 2, 2048, 256, 512
+S1 = S // 2
+COLS = B * D
+PASSES = S // 512
+CPASSES = S1 // 512
+FLOPS = 2 * COLS * (S1 * S + HZ * S + HZ * S1)
+BYTES = 2 * (B * S * D + S + S1 + HZ * S + HZ * S1 + HZ) + S1 * S + 4 * S + 4 * B * HZ * D
+
+
+def tile_timemixerpyramidforecast_kernel(tc, x, g0, w01_bytes, w01_scale, g1, f0, f1, ens, out):
+    nc = tc.nc
+    with ExitStack() as ctx:
+        keep = ctx.enter_context(tc.tile_pool(name="keep", bufs=1))
+        work = ctx.enter_context(tc.tile_pool(name="work", bufs=3))
+        psum = ctx.enter_context(tc.psum_pool(name="psum", bufs=1))
+
+        def kt(shape, dtype, name):
+            return keep.tile(shape, dtype, name=name, align_bytes=64)
+
+        g0_b = kt([P, PASSES, 4], BF16, "g0_b")
+        g1_b = kt([P, CPASSES, 4], BF16, "g1_b")
+        ens_b = kt([P, 4], BF16, "ens_b")
+        nc.scalar.dma_start(out=ens_b[:], in_=ens.rearrange("(m t) -> m t", t=4))
+        nc.scalar.dma_start(out=g0_b[:], in_=g0.rearrange("(g p t) -> p g t", p=P, t=4))
+        nc.scalar.dma_start(out=g1_b[:], in_=g1.rearrange("(g p t) -> p g t", p=P, t=4))
+
+        scale = kt([P, S], F32, "scale")
+        w_raw = [kt([P, S], U8, f"w_raw{j}") for j in range(8)]
+        x_fine = [kt([P, B, 4 * D], BF16, f"x_fine{g}") for g in range(PASSES)]
+        x_pair = [kt([P, B, 8 * D], BF16, f"x_pair{g}") for g in range(CPASSES)]
+        f0_raw = [kt([P, S], BF16, f"f0_raw{i}") for i in range(4)]
+        f1_raw = [kt([P, S1], BF16, f"f1_raw{i}") for i in range(4)]
+
+        scale_row = w01_scale.rearrange("o k -> (o k)")
+        w_rows = w01_bytes.rearrange("(g m t) k -> g t m k", g=2, t=4)
+        f0_rows = f0.rearrange("(m t) k -> t m k", t=4)
+        f1_rows = f1.rearrange("(m t) k -> t m k", t=4)
+
+        def load_scale(q):
+            nc.sync.dma_start(out=scale[:, q * 512 : (q + 1) * 512], in_=scale_row[q * 512 : (q + 1) * 512].partition_broadcast(P))
+
+        def load_w(j):
+            nc.sync.dma_start(out=w_raw[j][:], in_=w_rows[j // 4, j % 4])
+
+        def load_x(g):
+            nc.sync.dma_start(out=x_fine[g][:], in_=x[:, g * 512 : (g + 1) * 512, :].rearrange("b (p t) n -> p b (t n)", t=4))
+
+        def load_pair(g):
+            nc.sync.dma_start(out=x_pair[g][:], in_=x[:, g * 1024 : (g + 1) * 1024, :].rearrange("b (p t) n -> p b (t n)", t=8))
+
+        def load_f0(i):
+            nc.sync.dma_start(out=f0_raw[i][:], in_=f0_rows[i])
+
+        def load_f1(i):
+            nc.sync.dma_start(out=f1_raw[i][:], in_=f1_rows[i])
+
+
+        a_col = kt([P, 4], F32, "a_col")
+        na_col = kt([P, 4], F32, "na_col")
+        dummy = kt([P, 1], F32, "dummy")
+        zero = kt([P, 1], F32, "zero")
+        nc.vector.memset(zero[:], 0.0)
+        nc.scalar.activation(out=dummy[:], in_=zero[:], func=ACT.Sigmoid)
+        nc.scalar.activation(out=a_col[:], in_=ens_b[:], func=ACT.Sigmoid)
+        nc.scalar.activation(out=na_col[:], in_=ens_b[:], func=ACT.Sigmoid, scale=-1.0)
+        ident = kt([P, P], F32, "ident")
+        make_identity(nc, ident[:])
+        nc.scalar.activation(out=dummy[:], in_=zero[:], func=ACT.Gelu_apprx_tanh)
+        ident_b = kt([P, P], BF16, "ident_b")
+        nc.gpsimd.tensor_copy(out=ident_b[:], in_=ident[:])
+        g0_col = kt([P, PASSES, 4], F32, "g0_col")
+        g1_col = kt([P, CPASSES, 4], F32, "g1_col")
+        g1_half = kt([P, CPASSES, 4], F32, "g1_half")
+        nc.gpsimd.tensor_copy(out=g0_col[:], in_=g0_b[:])
+        nc.gpsimd.tensor_copy(out=g1_col[:], in_=g1_b[:])
+        nc.gpsimd.tensor_scalar(out=g1_half[:], in0=g1_b[:], scalar1=0.5, scalar2=0.0, op0=ALU.mult, op1=ALU.add)
+        d0 = kt([P, 4, P], BF16, "d0")
+        for t in range(4):
+            nc.gpsimd.tensor_scalar(out=d0[:, t, :], in0=ident_b[:], scalar1=g0_col[:, 3, t : t + 1], scalar2=0.0, op0=ALU.mult, op1=ALU.add)
+        dz = [kt([P, 4, P], BF16, f"dz{g}") for g in range(CPASSES)]
+        for g in range(CPASSES):
+            for t in range(4):
+                nc.gpsimd.tensor_scalar(out=dz[g][:, t, :], in0=ident_b[:], scalar1=g1_half[:, g, t : t + 1], scalar2=0.0, op0=ALU.mult, op1=ALU.add)
+
+        u_codes = [kt([P, COLS], U32, f"u_codes{g}") for g in range(PASSES)]
+        u_sc = [kt([P, COLS], U8, f"u_sc{g}") for g in range(PASSES)]
+        w_codes = [kt([P, PASSES * P], U32, f"w_codes{j}") for j in range(8)]
+        w_sc = [kt([P, PASSES * P], U8, f"w_sc{j}") for j in range(8)]
+        f0_codes = [kt([P, PASSES * P], U32, f"f0_codes{i}") for i in range(4)]
+        f0_sc = [kt([P, PASSES * P], U8, f"f0_sc{i}") for i in range(4)]
+        f1_codes = [kt([P, CPASSES * P], U32, f"f1_codes{i}") for i in range(4)]
+        f1_sc = [kt([P, CPASSES * P], U8, f"f1_sc{i}") for i in range(4)]
+        y_codes = [kt([P, COLS], U32, f"y_codes{g}") for g in range(CPASSES)]
+        y_sc = [kt([P, COLS], U8, f"y_sc{g}") for g in range(CPASSES)]
+        yp = [kt([P, 4, COLS], BF16, f"yp{g}") for g in range(CPASSES)]
+        h0_part = [kt([P, COLS], F32, f"h0_part{i}") for i in range(4)]
+        live = {}
+
+        depth = {"w_bf": 3, "w_g": 3, "f0_g": 4, "f1_g": 2, "u_g": 2, "y_g": 2}
+
+        def shared(name, n, width):
+            if (name, n) not in live:
+                live[name, n] = work.tile([P, width], BF16, name=name, bufs=depth[name], align_bytes=64)
+            return live[name, n]
+
+        def tp_bank():
+            return psum.tile([P, 2, 2, P], F32, name="tp", bufs=4)
+
+        def widen(j, h, chunks=1):
+            t = shared("w_bf", j, S)
+            n = S // 2 // chunks
+            for c in range(chunks):
+                cols = slice(h * (S // 2) + c * n, h * (S // 2) + (c + 1) * n)
+                nc.vector.tensor_tensor(out=t[:, cols], in0=w_raw[j][:, cols].bitcast(FP8), in1=scale[:, cols], op=ALU.mult)
+
+        def turn(src, half):
+            words = src[:].bitcast(F32)
+            bank = tp_bank()
+            for gg in range(2):
+                for u in range(2):
+                    lo = 256 * (2 * half + gg)
+                    nc.tensor.transpose(bank[:, gg, u, :], words[:, lo + u : lo + 256 : 2], ident[:])
+            return bank
+
+        def empty(dst, half, bank, eng):
+            o = dst[:, half * 1024 : (half + 1) * 1024].bitcast(F32).rearrange("p (g r u) -> p g r u", g=2, u=2)
+            i = bank[:].rearrange("p g u r -> p g r u")
+            if eng == "s":
+                nc.scalar.copy(out=o, in_=i)
+            else:
+                nc.vector.tensor_copy(out=o, in_=i)
+
+
+        def turn_w(j, h):
+            live["wt", j, h] = turn(live["w_bf", j], h)
+
+        def empty_w(j, h, eng="s"):
+            empty(shared("w_g", j, S), h, live["wt", j, h], eng)
+
+        def quant_w(j):
+            nc.vector.quantize_mx(out=w_codes[j][:].bitcast(FP8X4), scales=w_sc[j][:], in_=live["w_g", j][:])
+
+        def turn_f0(i, h):
+            live["f0t", i, h] = turn(f0_raw[i], h)
+
+        def empty_f0(i, h, eng="s"):
+            empty(shared("f0_g", i, S), h, live["f0t", i, h], eng)
+
+        def quant_f0(i):
+            nc.vector.quantize_mx(out=f0_codes[i][:].bitcast(FP8X4), scales=f0_sc[i][:], in_=live["f0_g", i][:])
+
+        def turn_f1(i):
+            live["f1t", i] = turn(f1_raw[i], 0)
+
+        def empty_f1(i, eng="s"):
+            empty(shared("f1_g", i, S1), 0, live["f1t", i], eng)
+
+        def quant_f1(i):
+            nc.vector.quantize_mx(out=f1_codes[i][:].bitcast(FP8X4), scales=f1_sc[i][:], in_=live["f1_g", i][:])
+
+        def gain(g):
+            t = work.tile([P, 4, COLS], BF16, name="x_s", bufs=2, align_bytes=64)
+            live["xs", g] = t
+            for k in range(4):
+                nc.vector.tensor_scalar(
+                    out=t[:, k, :].rearrange("p (b n) -> p b n", b=B),
+                    in0=x_fine[g][:, :, k * D : (k + 1) * D],
+                    scalar1=g0_col[:, g, k : k + 1],
+                    scalar2=None,
+                    op0=ALU.mult,
+                )
+
+        def weave(dst, src, eng, c0=0, c1=COLS):
+            o = dst[:].rearrange("p (c t) -> p c t", t=4)[:, c0:c1, :]
+            i = src[:].rearrange("p t c -> p c t")[:, c0:c1, :]
+            if eng == "s":
+                nc.scalar.copy(out=o, in_=i)
+            else:
+                nc.vector.tensor_copy(out=o, in_=i)
+
+        def weave_u(g, h, eng="s"):
+            weave(shared("u_g", g, 4 * COLS), live["xs", g], eng, h * D, (h + 1) * D)
+
+        def gain_mm(g, c):
+            bank = psum.tile([P, 4, P], F32, name="zh", bufs=2)
+            live["gb", g, c] = bank
+            b, n0 = c // 2, (c % 2) * P
+            for k in range(4):
+                nc.tensor.matmul(bank[:, k, :], lhsT=d0[:, k, :], rhs=x_fine[g][:, b, k * D + n0 : k * D + n0 + P], start=True, stop=True)
+
+        def gain_out(g, c, eng="s"):
+            o = shared("u_g", g, 4 * COLS)[:, c * 512 : (c + 1) * 512].rearrange("p (n t) -> p n t", t=4)
+            i = live["gb", g, c][:].rearrange("p t n -> p n t")
+            if eng == "s":
+                nc.scalar.copy(out=o, in_=i)
+            else:
+                nc.vector.tensor_copy(out=o, in_=i)
+
+        def quant_u(g):
+            nc.vector.quantize_mx(out=u_codes[g][:].bitcast(FP8X4), scales=u_sc[g][:], in_=live["u_g", g][:])
+
+        def mx(acc, codes, sc, mov, mov_sc, passes):
+            for g in range(passes):
+                nc.tensor.matmul_mx(
+                    out=acc[:],
+                    lhsT=codes[:, g * P : (g + 1) * P].bitcast(FP8X4),
+                    lhsT_scale=sc[:, g * P : (g + 1) * P],
+                    rhs=mov[g][:].bitcast(FP8X4),
+                    rhs_scale=mov_sc[g][:],
+                    start=(g == 0),
+                    stop=(g == passes - 1),
+                )
+
+        def mul_m(j):
+            acc = psum.tile([P, COLS], F32, name="m", bufs=2)
+            live["m", j] = acc
+            mx(acc, w_codes[j], w_sc[j], u_codes, u_sc, PASSES)
+
+        def gelu(j):
+            t = work.tile([P, COLS], F32, name="ge")
+            live["ge", j] = t
+            nc.scalar.activation(out=t[:], in_=live["m", j][:], func=ACT.Gelu_apprx_tanh)
+
+        def pair(j):
+            g, k = j // 4, j % 4
+            acc = psum.tile([P, COLS], F32, name="zh", bufs=2)
+            live["z", j] = acc
+            for e in range(2):
+                s = 2 * k + e
+                nc.tensor.matmul(acc[:].rearrange("p (b n) -> p b n", b=B), lhsT=dz[g][:, k, :], rhs=x_pair[g][:, :, s * D : (s + 1) * D], start=(e == 0), stop=(e == 1))
+
+        def mix(j):
+            g, k = j // 4, j % 4
+            nc.vector.scalar_tensor_tensor(out=yp[g][:, k, :], in0=live["ge", j][:], scalar=g1_col[:, g, k : k + 1], in1=live["z", j][:], op0=ALU.mult, op1=ALU.add)
+
+        def weave_y(g, q, eng):
+            weave(shared("y_g", g, 4 * COLS), yp[g], eng, q * P, (q + 1) * P)
+
+        def quant_y(g):
+            nc.vector.quantize_mx(out=y_codes[g][:].bitcast(FP8X4), scales=y_sc[g][:], in_=live["y_g", g][:])
+
+        def mul_h0(i):
+            acc = psum.tile([P, COLS], F32, name="zh", bufs=2)
+            live["h0", i] = acc
+            mx(acc, f0_codes[i], f0_sc[i], u_codes, u_sc, PASSES)
+
+        def keep_h0(i):
+            nc.scalar.activation(out=h0_part[i][:], in_=live["h0", i][:], func=ACT.Copy, scale=a_col[:, i : i + 1])
+
+        def mul_h1(i):
+            acc = psum.tile([P, COLS], F32, name=("zh", "m")[i % 2], bufs=2)
+            live["h1", i] = acc
+            mx(acc, f1_codes[i], f1_sc[i], y_codes, y_sc, CPASSES)
+
+        out_rows = out.rearrange("b (m t) n -> t m b n", t=4)
+
+        def blend(i):
+            o = work.tile([P, B, D], F32, name="o")
+            nc.vector.scalar_tensor_tensor(out=o[:].rearrange("p b n -> p (b n)"), in0=live["h1", i][:], scalar=na_col[:, i : i + 1], in1=h0_part[i][:], op0=ALU.mult, op1=ALU.add)
+            nc.sync.dma_start(out=out_rows[i], in_=o[:])
+
+        with tc.manual_schedule(engines={mybir.EngineType.PE, mybir.EngineType.DVE, mybir.EngineType.Activation}):
+            load_x(1)
+            gain(1)
+            weave_u(1, 1, "s")
+            weave_u(1, 0, "s")
+            load_scale(0)
+            load_w(0)
+            load_scale(1)
+            widen(0, 0, 2)
+            load_w(3)
+            load_f1(2)
+            load_scale(2)
+            widen(3, 0)
+            load_scale(3)
+            turn_w(0, 0)
+            load_w(2)
+            turn_f1(2)
+            widen(0, 1, 2)
+            turn_w(3, 0)
+            turn_w(0, 1)
+            empty_w(0, 0, "s")
+            empty_f1(2, "s")
+            empty_w(3, 0, "s")
+            widen(2, 1)
+            empty_w(0, 1, "s")
+            load_x(3)
+            gain_mm(3, 2)
+            widen(2, 0)
+            gain_mm(3, 0)
+            load_x(0)
+            gain(0)
+            load_w(1)
+            gain_out(3, 2, "s")
+            turn_w(2, 1)
+            gain_out(3, 0, "s")
+            gain_mm(3, 3)
+            empty_w(2, 1, "s")
+            turn_w(2, 0)
+            gain_mm(3, 1)
+            gain_out(3, 3, "s")
+            load_f0(2)
+            turn_f0(2, 1)
+            empty_w(2, 0, "s")
+            quant_u(1)
+            widen(3, 1)
+            widen(1, 1)
+            load_w(4)
+            load_f0(1)
+            gain_out(3, 1, "s")
+            quant_w(0)
+            quant_u(3)
+            weave_u(0, 1, "s")
+            load_pair(0)
+            widen(1, 0)
+            load_f1(0)
+            turn_w(3, 1)
+            turn_w(1, 1)
+            turn_f0(1, 0)
+            empty_f0(2, 1, "s")
+            pair(2)
+            empty_w(3, 1, "s")
+            turn_f0(1, 1)
+            widen(4, 1)
+            load_f0(0)
+            turn_f0(0, 0)
+            quant_w(3)
+            empty_w(1, 1, "s")
+            weave_u(0, 0, "s")
+            load_x(2)
+            turn_w(4, 1)
+            load_w(6)
+            empty_f0(1, 0, "s")
+            quant_u(0)
+            gain(2)
+            empty_f0(1, 1, "s")
+            pair(0)
+            empty_f0(0, 0, "s")
+            turn_w(1, 0)
+            empty_w(4, 1, "s")
+            empty_w(1, 0, "s")
+            widen(4, 0)
+            turn_f1(0)
+            turn_f0(0, 1)
+            load_w(7)
+            weave_u(2, 0, "v")
+            quant_w(2)
+            weave_u(2, 1, "s")
+            turn_w(4, 0)
+            quant_u(2)
+            turn_f0(2, 0)
+            empty_w(4, 0, "s")
+            quant_w(1)
+            load_w(5)
+            mul_m(2)
+            gelu(2)
+            mul_m(0)
+            gelu(0)
+            widen(6, 0)
+            mix(2)
+            mul_m(3)
+            empty_f0(0, 1, "s")
+            mul_m(1)
+            widen(7, 1)
+            empty_f1(0, "s")
+            load_f0(3)
+            pair(3)
+            turn_f0(3, 0)
+            widen(7, 0)
+            widen(5, 0)
+            turn_w(7, 0)
+            empty_f0(2, 0, "s")
+            turn_w(7, 1)
+            empty_f0(3, 0, "s")
+            widen(5, 1)
+            empty_w(7, 0, "s")
+            empty_w(7, 1, "s")
+            turn_f0(3, 1)
+            empty_f0(3, 1, "s")
+            turn_w(6, 0)
+            turn_w(5, 1)
+            turn_w(5, 0)
+            gelu(3)
+            widen(6, 1)
+            empty_w(5, 1, "s")
+            turn_w(6, 1)
+            gelu(1)
+            quant_w(7)
+            mix(0)
+            quant_w(4)
+            quant_f0(3)
+            load_pair(1)
+            mul_m(7)
+            pair(1)
+            quant_f1(2)
+            mix(3)
+            empty_w(5, 0, "s")
+            quant_w(5)
+            load_f1(3)
+            empty_w(6, 1, "s")
+            mix(1)
+            empty_w(6, 0, "s")
+            quant_w(6)
+            mul_m(4)
+            gelu(7)
+            weave_y(0, 3, "s")
+            gelu(4)
+            pair(7)
+            mix(7)
+            mul_m(5)
+            quant_f0(2)
+            load_f1(1)
+            quant_f1(0)
+            gelu(5)
+            pair(5)
+            mix(5)
+            pair(4)
+            mul_m(6)
+            weave_y(0, 2, "s")
+            mix(4)
+            pair(6)
+            quant_f0(1)
+            weave_y(0, 0, "s")
+            gelu(6)
+            mix(6)
+            mul_h0(2)
+            quant_f0(0)
+            weave_y(0, 1, "s")
+            weave_y(1, 0, "v")
+            mul_h0(1)
+            weave_y(1, 3, "s")
+            weave_y(1, 2, "v")
+            weave_y(1, 1, "s")
+            quant_y(0)
+            turn_f1(1)
+            quant_y(1)
+            turn_f1(3)
+            keep_h0(2)
+            mul_h1(2)
+            keep_h0(1)
+            blend(2)
+            empty_f1(1, "s")
+            quant_f1(1)
+            empty_f1(3, "s")
+            mul_h0(0)
+            mul_h0(3)
+            keep_h0(0)
+            quant_f1(3)
+            keep_h0(3)
+            mul_h1(0)
+            blend(0)
+            mul_h1(3)
+            blend(3)
+            mul_h1(1)
+            blend(1)

@@ -32,12 +32,14 @@ def tile_timemixerpyramidforecast_kernel(tc, x, g0, w01_bytes, w01_scale, g1, f0
         def kt(shape, dtype, name):
             return keep.tile(shape, dtype, name=name, align_bytes=64)
 
-        g0_b = kt([P, PASSES, 4], BF16, "g0_b")
-        g1_b = kt([P, CPASSES, 4], BF16, "g1_b")
-        ens_b = kt([P, 4], BF16, "ens_b")
-        nc.scalar.dma_start(out=ens_b[:], in_=ens.rearrange("(m t) -> m t", t=4))
-        nc.scalar.dma_start(out=g0_b[:], in_=g0.rearrange("(g p t) -> p g t", p=P, t=4))
-        nc.scalar.dma_start(out=g1_b[:], in_=g1.rearrange("(g p t) -> p g t", p=P, t=4))
+        s_rows = kt([P, P], F32, "s_rows")
+        c_rows = kt([P, 512], BF16, "c_rows")
+        nc.vector.memset(s_rows[:], 0.0)
+        nc.vector.memset(c_rows[:], 0.0)
+        nc.scalar.dma_start(out=s_rows[0:16, :], in_=w01_scale.rearrange("o (m n) -> (o m) n", n=P))
+        nc.scalar.dma_start(out=c_rows[0:4, :], in_=g0.rearrange("(g k) -> g k", k=512))
+        nc.scalar.dma_start(out=c_rows[4:6, :], in_=g1.rearrange("(g k) -> g k", k=512))
+        nc.scalar.dma_start(out=c_rows[6:7, :], in_=ens.rearrange("(g k) -> g k", k=512))
 
         scale = kt([P, S], F32, "scale")
         w_raw = [kt([P, S], U8, f"w_raw{j}") for j in range(8)]
@@ -46,13 +48,9 @@ def tile_timemixerpyramidforecast_kernel(tc, x, g0, w01_bytes, w01_scale, g1, f0
         f0_raw = [kt([P, S], BF16, f"f0_raw{i}") for i in range(4)]
         f1_raw = [kt([P, S1], BF16, f"f1_raw{i}") for i in range(4)]
 
-        scale_row = w01_scale.rearrange("o k -> (o k)")
         w_rows = w01_bytes.rearrange("(g m t) k -> g t m k", g=2, t=4)
         f0_rows = f0.rearrange("(m t) k -> t m k", t=4)
         f1_rows = f1.rearrange("(m t) k -> t m k", t=4)
-
-        def load_scale(q):
-            nc.sync.dma_start(out=scale[:, q * 512 : (q + 1) * 512], in_=scale_row[q * 512 : (q + 1) * 512].partition_broadcast(P))
 
         def load_w(j):
             nc.sync.dma_start(out=w_raw[j][:], in_=w_rows[j // 4, j % 4])
@@ -76,26 +74,18 @@ def tile_timemixerpyramidforecast_kernel(tc, x, g0, w01_bytes, w01_scale, g1, f0
         zero = kt([P, 1], F32, "zero")
         nc.vector.memset(zero[:], 0.0)
         nc.scalar.activation(out=dummy[:], in_=zero[:], func=ACT.Sigmoid)
-        nc.scalar.activation(out=a_col[:], in_=ens_b[:], func=ACT.Sigmoid)
-        nc.scalar.activation(out=na_col[:], in_=ens_b[:], func=ACT.Sigmoid, scale=-1.0)
         ident = kt([P, P], F32, "ident")
         make_identity(nc, ident[:])
-        nc.scalar.activation(out=dummy[:], in_=zero[:], func=ACT.Gelu_apprx_tanh)
         ident_b = kt([P, P], BF16, "ident_b")
         nc.gpsimd.tensor_copy(out=ident_b[:], in_=ident[:])
-        g0_col = kt([P, PASSES, 4], F32, "g0_col")
-        g1_col = kt([P, CPASSES, 4], F32, "g1_col")
+        s_cols = kt([P, 16], F32, "s_cols")
+        c_words = kt([P, 2, 8], F32, "c_words")
+        cols = kt([P, 8, 4], F32, "cols")
         g1_half = kt([P, CPASSES, 4], F32, "g1_half")
-        nc.gpsimd.tensor_copy(out=g0_col[:], in_=g0_b[:])
-        nc.gpsimd.tensor_copy(out=g1_col[:], in_=g1_b[:])
-        nc.gpsimd.tensor_scalar(out=g1_half[:], in0=g1_b[:], scalar1=0.5, scalar2=0.0, op0=ALU.mult, op1=ALU.add)
         d0 = kt([P, 4, P], BF16, "d0")
-        for t in range(4):
-            nc.gpsimd.tensor_scalar(out=d0[:, t, :], in0=ident_b[:], scalar1=g0_col[:, 3, t : t + 1], scalar2=0.0, op0=ALU.mult, op1=ALU.add)
         dz = [kt([P, 4, P], BF16, f"dz{g}") for g in range(CPASSES)]
-        for g in range(CPASSES):
-            for t in range(4):
-                nc.gpsimd.tensor_scalar(out=dz[g][:, t, :], in0=ident_b[:], scalar1=g1_half[:, g, t : t + 1], scalar2=0.0, op0=ALU.mult, op1=ALU.add)
+        g0_col = cols[:, 0:4, :]
+        g1_col = cols[:, 4:6, :]
 
         u_codes = [kt([P, COLS], U32, f"u_codes{g}") for g in range(PASSES)]
         u_sc = [kt([P, COLS], U8, f"u_sc{g}") for g in range(PASSES)]
@@ -120,6 +110,57 @@ def tile_timemixerpyramidforecast_kernel(tc, x, g0, w01_bytes, w01_scale, g1, f0
 
         def tp_bank():
             return psum.tile([P, 2, 2, P], F32, name="tp", bufs=4)
+
+        def turn_consts():
+            bank = tp_bank()
+            live["consts"] = bank
+            words = c_rows[:].bitcast(F32)
+            nc.tensor.transpose(bank[:, 0, 0, :], s_rows[:], ident[:])
+            for u in range(2):
+                nc.tensor.transpose(bank[:, 1, u, :], words[:, u:256:2], ident[:])
+
+        def fetch_consts():
+            bank = live["consts"]
+            nc.vector.tensor_copy(out=s_cols[:], in_=bank[:, 0, 0, 0:16])
+            nc.vector.tensor_copy(out=c_words[:], in_=bank[:, 1, :, 0:8])
+            nc.vector.tensor_copy(
+                out=cols[:].rearrange("p r (u e) -> p r u e", u=2),
+                in_=c_words[:].rearrange("p u r -> p (u r)").bitcast(BF16).rearrange("p (u r e) -> p r u e", u=2, e=2),
+            )
+            nc.vector.tensor_scalar(out=g1_half[:], in0=g1_col, scalar1=0.5, scalar2=None, op0=ALU.mult)
+
+        def weights():
+            nc.scalar.activation(out=a_col[:], in_=cols[:, 6, :], func=ACT.Sigmoid)
+            nc.scalar.activation(out=na_col[:], in_=cols[:, 6, :], func=ACT.Sigmoid, scale=-1.0)
+
+        def gelu_table():
+            nc.scalar.activation(out=dummy[:], in_=zero[:], func=ACT.Gelu_apprx_tanh)
+
+        def spread(q):
+            bank = tp_bank()
+            live["spread", q] = bank
+            for i in range(4):
+                nc.tensor.transpose(bank[:, i // 2, i % 2, :], s_cols[:, 4 * q + i : 4 * q + i + 1].to_broadcast([P, P]), ident[:])
+
+        def spread_out(q, eng="s"):
+            o = scale[:, 512 * q : 512 * (q + 1)]
+            i = live["spread", q][:].rearrange("p g u n -> p (g u n)")
+            if eng == "s":
+                nc.scalar.copy(out=o, in_=i)
+            else:
+                nc.vector.tensor_copy(out=o, in_=i)
+
+        def diag(dst, t, col, eng):
+            if eng == "s":
+                nc.scalar.activation(out=dst[:, t, :], in_=ident_b[:], func=ACT.Copy, scale=col)
+            else:
+                nc.vector.tensor_scalar(out=dst[:, t, :], in0=ident_b[:], scalar1=col, scalar2=None, op0=ALU.mult)
+
+        def diag_x(t, eng="v"):
+            diag(d0, t, g0_col[:, 3, t : t + 1], eng)
+
+        def diag_z(j, eng="v"):
+            diag(dz[j // 4], j % 4, g1_half[:, j // 4, j % 4 : j % 4 + 1], eng)
 
         def widen(j, h, chunks=1):
             t = shared("w_bf", j, S)
@@ -275,195 +316,215 @@ def tile_timemixerpyramidforecast_kernel(tc, x, g0, w01_bytes, w01_scale, g1, f0
             nc.sync.dma_start(out=out_rows[i], in_=o[:])
 
         with tc.manual_schedule(engines={mybir.EngineType.PE, mybir.EngineType.DVE, mybir.EngineType.Activation}):
+            turn_consts()
+            fetch_consts()
+            spread(0)
+            diag_x(1, "s")
             load_x(1)
-            gain(1)
-            weave_u(1, 1, "s")
-            weave_u(1, 0, "s")
-            load_scale(0)
-            load_w(0)
-            load_scale(1)
-            widen(0, 0, 2)
-            load_w(3)
-            load_f1(2)
-            load_scale(2)
-            widen(3, 0)
-            load_scale(3)
-            turn_w(0, 0)
-            load_w(2)
-            turn_f1(2)
-            widen(0, 1, 2)
-            turn_w(3, 0)
-            turn_w(0, 1)
-            empty_w(0, 0, "s")
-            empty_f1(2, "s")
-            empty_w(3, 0, "s")
-            widen(2, 1)
-            empty_w(0, 1, "s")
-            load_x(3)
-            gain_mm(3, 2)
-            widen(2, 0)
-            gain_mm(3, 0)
-            load_x(0)
-            gain(0)
-            load_w(1)
-            gain_out(3, 2, "s")
-            turn_w(2, 1)
-            gain_out(3, 0, "s")
-            gain_mm(3, 3)
-            empty_w(2, 1, "s")
-            turn_w(2, 0)
-            gain_mm(3, 1)
-            gain_out(3, 3, "s")
-            load_f0(2)
-            turn_f0(2, 1)
-            empty_w(2, 0, "s")
-            quant_u(1)
-            widen(3, 1)
-            widen(1, 1)
-            load_w(4)
-            load_f0(1)
-            gain_out(3, 1, "s")
-            quant_w(0)
-            quant_u(3)
-            weave_u(0, 1, "s")
-            load_pair(0)
-            widen(1, 0)
             load_f1(0)
-            turn_w(3, 1)
-            turn_w(1, 1)
-            turn_f0(1, 0)
-            empty_f0(2, 1, "s")
-            pair(2)
-            empty_w(3, 1, "s")
-            turn_f0(1, 1)
-            widen(4, 1)
-            load_f0(0)
-            turn_f0(0, 0)
-            quant_w(3)
-            empty_w(1, 1, "s")
-            weave_u(0, 0, "s")
-            load_x(2)
-            turn_w(4, 1)
-            load_w(6)
-            empty_f0(1, 0, "s")
-            quant_u(0)
-            gain(2)
-            empty_f0(1, 1, "s")
-            pair(0)
-            empty_f0(0, 0, "s")
-            turn_w(1, 0)
-            empty_w(4, 1, "s")
-            empty_w(1, 0, "s")
-            widen(4, 0)
+            load_w(0)
+            load_x(0)
+            load_f0(1)
+            diag_x(2, "v")
+            spread(1)
+            diag_z(3, "s")
+            load_w(1)
+            spread_out(0, "v")
+            load_w(3)
+            diag_x(3, "s")
+            diag_x(0, "s")
+            gain(1)
+            spread_out(1, "s")
+            widen(0, 0, 2)
+            spread(2)
+            spread_out(2, "s")
+            spread(3)
+            gain(0)
             turn_f1(0)
-            turn_f0(0, 1)
-            load_w(7)
-            weave_u(2, 0, "v")
-            quant_w(2)
-            weave_u(2, 1, "s")
-            turn_w(4, 0)
-            quant_u(2)
-            turn_f0(2, 0)
-            empty_w(4, 0, "s")
-            quant_w(1)
-            load_w(5)
-            mul_m(2)
-            gelu(2)
-            mul_m(0)
-            gelu(0)
-            widen(6, 0)
-            mix(2)
-            mul_m(3)
-            empty_f0(0, 1, "s")
-            mul_m(1)
-            widen(7, 1)
+            spread_out(3, "s")
+            widen(0, 1, 2)
+            diag_z(0, "s")
+            weights()
+            widen(1, 0)
+            widen(3, 0)
             empty_f1(0, "s")
+            turn_f0(1, 1)
             load_f0(3)
-            pair(3)
-            turn_f0(3, 0)
-            widen(7, 0)
-            widen(5, 0)
-            turn_w(7, 0)
+            load_x(3)
+            weave_u(1, 0, "s")
+            turn_w(0, 0)
+            empty_w(0, 0, "s")
+            weave_u(0, 0, "v")
+            load_x(2)
+            empty_f0(1, 1, "s")
+            load_w(5)
+            weave_u(1, 1, "s")
+            load_f0(2)
+            turn_f0(1, 0)
+            turn_w(0, 1)
+            quant_u(1)
+            empty_w(0, 1, "s")
+            empty_f0(1, 0, "s")
+            weave_u(0, 1, "s")
+            load_w(4)
+            gain(2)
+            load_w(7)
+            turn_w(1, 0)
+            gain_mm(3, 3)
+            turn_f0(2, 0)
+            load_w(6)
+            gain_out(3, 3, "s")
+            empty_w(1, 0, "s")
             empty_f0(2, 0, "s")
-            turn_w(7, 1)
-            empty_f0(3, 0, "s")
-            widen(5, 1)
-            empty_w(7, 0, "s")
-            empty_w(7, 1, "s")
+            widen(3, 1)
             turn_f0(3, 1)
+            load_w(2)
+            quant_w(0)
+            turn_f0(3, 0)
+            empty_f0(3, 0, "s")
             empty_f0(3, 1, "s")
+            load_f0(0)
+            quant_u(0)
+            widen(1, 1)
+            widen(2, 1)
+            gain_mm(3, 2)
+            weave_u(2, 1, "v")
+            gain_out(3, 2, "s")
+            turn_w(3, 1)
+            turn_f0(2, 1)
+            turn_w(1, 1)
+            empty_w(3, 1, "s")
+            load_pair(0)
+            empty_f0(2, 1, "s")
+            empty_w(1, 1, "s")
+            gain_mm(3, 0)
+            turn_w(2, 1)
+            load_f1(3)
+            load_pair(1)
+            empty_w(2, 1, "s")
+            gain_mm(3, 1)
+            widen(7, 0)
+            turn_f0(0, 0)
+            turn_w(3, 0)
+            widen(7, 1)
+            gain_out(3, 0, "s")
+            turn_w(7, 0)
+            pair(0)
+            gain_out(3, 1, "s")
+            pair(3)
+            empty_f0(0, 0, "s")
+            turn_f0(0, 1)
+            quant_w(1)
+            weave_u(2, 0, "s")
+            widen(2, 0)
+            turn_w(2, 0)
+            quant_u(3)
+            quant_u(2)
+            empty_w(3, 0, "s")
+            gelu_table()
+            diag_z(1, "s")
+            quant_w(3)
+            mul_m(0)
+            widen(6, 0)
+            turn_w(7, 1)
+            gelu(0)
+            empty_f0(0, 1, "s")
+            widen(6, 1)
+            mul_m(1)
+            empty_w(7, 0, "s")
+            mul_m(3)
+            empty_w(2, 0, "s")
+            widen(4, 0)
+            load_f1(2)
+            turn_w(6, 1)
+            empty_w(7, 1, "s")
+            load_f1(1)
             turn_w(6, 0)
+            empty_w(6, 1, "s")
+            widen(5, 1)
+            empty_w(6, 0, "s")
+            turn_w(4, 0)
+            turn_f1(2)
+            gelu(1)
             turn_w(5, 1)
+            turn_f1(3)
+            quant_w(2)
+            mul_m(2)
+            diag_z(6, "s")
+            diag_z(7, "s")
+            widen(5, 0)
+            empty_w(4, 0, "s")
+            widen(4, 1)
+            empty_f1(2, "s")
+            diag_z(2, "s")
+            turn_w(4, 1)
+            quant_w(7)
             turn_w(5, 0)
             gelu(3)
-            widen(6, 1)
-            empty_w(5, 1, "s")
-            turn_w(6, 1)
-            gelu(1)
-            quant_w(7)
             mix(0)
-            quant_w(4)
-            quant_f0(3)
-            load_pair(1)
-            mul_m(7)
-            pair(1)
-            quant_f1(2)
-            mix(3)
             empty_w(5, 0, "s")
-            quant_w(5)
-            load_f1(3)
-            empty_w(6, 1, "s")
-            mix(1)
-            empty_w(6, 0, "s")
+            mix(3)
+            mul_m(7)
+            quant_f0(2)
             quant_w(6)
-            mul_m(4)
+            empty_w(5, 1, "s")
+            pair(1)
+            pair(2)
+            gelu(2)
+            quant_f0(0)
+            mul_m(6)
+            mix(1)
+            quant_w(5)
+            diag_z(5, "s")
+            mix(2)
+            empty_w(4, 1, "s")
             gelu(7)
-            weave_y(0, 3, "s")
-            gelu(4)
+            pair(6)
+            quant_w(4)
+            gelu(6)
+            mix(6)
+            weave_y(0, 0, "s")
+            quant_f0(3)
+            mul_m(5)
             pair(7)
             mix(7)
-            mul_m(5)
-            quant_f0(2)
-            load_f1(1)
-            quant_f1(0)
             gelu(5)
             pair(5)
             mix(5)
-            pair(4)
-            mul_m(6)
-            weave_y(0, 2, "s")
-            mix(4)
-            pair(6)
-            quant_f0(1)
-            weave_y(0, 0, "s")
-            gelu(6)
-            mix(6)
-            mul_h0(2)
-            quant_f0(0)
             weave_y(0, 1, "s")
-            weave_y(1, 0, "v")
-            mul_h0(1)
-            weave_y(1, 3, "s")
+            diag_z(4, "s")
+            weave_y(0, 3, "s")
+            mul_m(4)
+            gelu(4)
+            quant_f1(2)
+            quant_f1(0)
+            pair(4)
+            mul_h0(3)
+            mix(4)
+            weave_y(0, 2, "s")
             weave_y(1, 2, "v")
+            keep_h0(3)
             weave_y(1, 1, "s")
+            weave_y(1, 3, "v")
+            weave_y(1, 0, "v")
+            mul_h0(0)
+            keep_h0(0)
+            empty_f1(3, "s")
+            mul_h0(2)
             quant_y(0)
-            turn_f1(1)
             quant_y(1)
-            turn_f1(3)
             keep_h0(2)
-            mul_h1(2)
-            keep_h0(1)
-            blend(2)
+            mul_h1(0)
+            quant_f0(1)
+            blend(0)
+            quant_f1(3)
+            turn_f1(1)
             empty_f1(1, "s")
             quant_f1(1)
-            empty_f1(3, "s")
-            mul_h0(0)
-            mul_h0(3)
-            keep_h0(0)
-            quant_f1(3)
-            keep_h0(3)
-            mul_h1(0)
-            blend(0)
+            mul_h0(1)
+            keep_h0(1)
+            mul_h1(2)
+            blend(2)
             mul_h1(3)
             blend(3)
             mul_h1(1)

@@ -33,13 +33,10 @@ def tile_timemixerpyramidforecast_kernel(tc, x, g0, w01_bytes, w01_scale, g1, f0
             return keep.tile(shape, dtype, name=name, align_bytes=64)
 
         s_rows = kt([P, P], F32, "s_rows")
-        c_rows = kt([P, 512], BF16, "c_rows")
-        nc.vector.memset(s_rows[:], 0.0)
-        nc.vector.memset(c_rows[:], 0.0)
-        nc.scalar.dma_start(out=s_rows[0:16, :], in_=w01_scale.rearrange("o (m n) -> (o m) n", n=P))
-        nc.scalar.dma_start(out=c_rows[0:4, :], in_=g0.rearrange("(g k) -> g k", k=512))
-        nc.scalar.dma_start(out=c_rows[4:6, :], in_=g1.rearrange("(g k) -> g k", k=512))
-        nc.scalar.dma_start(out=c_rows[6:7, :], in_=ens.rearrange("(g k) -> g k", k=512))
+        g0_col = kt([P, PASSES, 4], BF16, "g0_col")
+        g1_col = kt([P, CPASSES, 4], BF16, "g1_col")
+        ens_col = kt([P, 4], BF16, "ens_col")
+        nc.gpsimd.memset(s_rows[:], 0.0)
 
         scale = kt([P, S], F32, "scale")
         w_raw = [kt([P, S], U8, f"w_raw{j}") for j in range(8)]
@@ -51,6 +48,14 @@ def tile_timemixerpyramidforecast_kernel(tc, x, g0, w01_bytes, w01_scale, g1, f0
         w_rows = w01_bytes.rearrange("(g m t) k -> g t m k", g=2, t=4)
         f0_rows = f0.rearrange("(m t) k -> t m k", t=4)
         f1_rows = f1.rearrange("(m t) k -> t m k", t=4)
+
+        def load_consts():
+            nc.sync.dma_start(out=s_rows[0:16, :], in_=w01_scale.rearrange("o (m n) -> (o m) n", n=P))
+            nc.sync.dma_start(out=g0_col[:], in_=g0.rearrange("(g p t) -> p g t", p=P, t=4))
+
+        def load_late():
+            nc.sync.dma_start(out=g1_col[:], in_=g1.rearrange("(g p t) -> p g t", p=P, t=4))
+            nc.sync.dma_start(out=ens_col[:], in_=ens.rearrange("(m t) -> m t", t=4))
 
         def load_w(j):
             nc.sync.dma_start(out=w_raw[j][:], in_=w_rows[j // 4, j % 4])
@@ -73,19 +78,16 @@ def tile_timemixerpyramidforecast_kernel(tc, x, g0, w01_bytes, w01_scale, g1, f0
         dummy = kt([P, 1], F32, "dummy")
         zero = kt([P, 1], F32, "zero")
         nc.vector.memset(zero[:], 0.0)
-        nc.scalar.activation(out=dummy[:], in_=zero[:], func=ACT.Sigmoid)
+        nc.scalar.activation(out=dummy[:], in_=zero[:], func=ACT.Gelu_apprx_tanh)
         ident = kt([P, P], F32, "ident")
         make_identity(nc, ident[:])
         ident_b = kt([P, P], BF16, "ident_b")
         nc.gpsimd.tensor_copy(out=ident_b[:], in_=ident[:])
         s_cols = kt([P, 16], F32, "s_cols")
-        c_words = kt([P, 2, 8], F32, "c_words")
-        cols = kt([P, 8, 4], F32, "cols")
+        th_col = kt([P, 4], F32, "th_col")
         g1_half = kt([P, CPASSES, 4], F32, "g1_half")
         d0 = kt([P, 4, P], BF16, "d0")
         dz = [kt([P, 4, P], BF16, f"dz{g}") for g in range(CPASSES)]
-        g0_col = cols[:, 0:4, :]
-        g1_col = cols[:, 4:6, :]
 
         u_codes = [kt([P, COLS], U32, f"u_codes{g}") for g in range(PASSES)]
         u_sc = [kt([P, COLS], U8, f"u_sc{g}") for g in range(PASSES)]
@@ -114,27 +116,18 @@ def tile_timemixerpyramidforecast_kernel(tc, x, g0, w01_bytes, w01_scale, g1, f0
         def turn_consts():
             bank = tp_bank()
             live["consts"] = bank
-            words = c_rows[:].bitcast(F32)
             nc.tensor.transpose(bank[:, 0, 0, :], s_rows[:], ident[:])
-            for u in range(2):
-                nc.tensor.transpose(bank[:, 1, u, :], words[:, u:256:2], ident[:])
 
-        def fetch_consts():
-            bank = live["consts"]
-            nc.vector.tensor_copy(out=s_cols[:], in_=bank[:, 0, 0, 0:16])
-            nc.vector.tensor_copy(out=c_words[:], in_=bank[:, 1, :, 0:8])
-            nc.vector.tensor_copy(
-                out=cols[:].rearrange("p r (u e) -> p r u e", u=2),
-                in_=c_words[:].rearrange("p u r -> p (u r)").bitcast(BF16).rearrange("p (u r e) -> p r u e", u=2, e=2),
-            )
-            nc.vector.tensor_scalar(out=g1_half[:], in0=g1_col, scalar1=0.5, scalar2=None, op0=ALU.mult)
+        def fetch_scales():
+            nc.scalar.copy(out=s_cols[:], in_=live["consts"][:, 0, 0, 0:16])
+
+        def halve_gains():
+            nc.gpsimd.tensor_scalar(out=g1_half[:], in0=g1_col[:], scalar1=0.5, scalar2=0.0, op0=ALU.mult, op1=ALU.add)
 
         def weights():
-            nc.scalar.activation(out=a_col[:], in_=cols[:, 6, :], func=ACT.Sigmoid)
-            nc.scalar.activation(out=na_col[:], in_=cols[:, 6, :], func=ACT.Sigmoid, scale=-1.0)
-
-        def gelu_table():
-            nc.scalar.activation(out=dummy[:], in_=zero[:], func=ACT.Gelu_apprx_tanh)
+            nc.scalar.activation(out=th_col[:], in_=ens_col[:], func=ACT.Tanh, scale=0.5)
+            nc.gpsimd.tensor_scalar(out=a_col[:], in0=th_col[:], scalar1=0.5, scalar2=0.5, op0=ALU.mult, op1=ALU.add)
+            nc.gpsimd.tensor_scalar(out=na_col[:], in0=th_col[:], scalar1=-0.5, scalar2=0.5, op0=ALU.mult, op1=ALU.add)
 
         def spread(q):
             bank = tp_bank()
@@ -310,222 +303,234 @@ def tile_timemixerpyramidforecast_kernel(tc, x, g0, w01_bytes, w01_scale, g1, f0
 
         out_rows = out.rearrange("b (m t) n -> t m b n", t=4)
 
-        def blend(i):
+        def blend(i, pieces=1):
             o = work.tile([P, B, D], F32, name="o")
-            nc.vector.scalar_tensor_tensor(out=o[:].rearrange("p b n -> p (b n)"), in0=live["h1", i][:], scalar=na_col[:, i : i + 1], in1=h0_part[i][:], op0=ALU.mult, op1=ALU.add)
-            nc.sync.dma_start(out=out_rows[i], in_=o[:])
+            n = B // pieces
+            for c in range(pieces):
+                cols_c = slice(c * n * D, (c + 1) * n * D)
+                nc.vector.scalar_tensor_tensor(
+                    out=o[:].rearrange("p b n -> p (b n)")[:, cols_c],
+                    in0=live["h1", i][:, cols_c],
+                    scalar=na_col[:, i : i + 1],
+                    in1=h0_part[i][:, cols_c],
+                    op0=ALU.mult,
+                    op1=ALU.add,
+                )
+                nc.sync.dma_start(out=out_rows[i][:, c * n : (c + 1) * n, :], in_=o[:, c * n : (c + 1) * n, :])
 
         with tc.manual_schedule(engines={mybir.EngineType.PE, mybir.EngineType.DVE, mybir.EngineType.Activation}):
+            load_consts()
             turn_consts()
-            fetch_consts()
-            spread(0)
-            diag_x(1, "s")
-            load_x(1)
-            load_f1(0)
-            load_w(0)
-            load_x(0)
-            load_f0(1)
             diag_x(2, "v")
-            spread(1)
-            diag_z(3, "s")
-            load_w(1)
-            spread_out(0, "v")
-            load_w(3)
-            diag_x(3, "s")
-            diag_x(0, "s")
-            gain(1)
-            spread_out(1, "s")
-            widen(0, 0, 2)
-            spread(2)
-            spread_out(2, "s")
+            fetch_scales()
             spread(3)
-            gain(0)
-            turn_f1(0)
             spread_out(3, "s")
-            widen(0, 1, 2)
-            diag_z(0, "s")
-            weights()
-            widen(1, 0)
-            widen(3, 0)
-            empty_f1(0, "s")
-            turn_f0(1, 1)
-            load_f0(3)
-            load_x(3)
-            weave_u(1, 0, "s")
-            turn_w(0, 0)
-            empty_w(0, 0, "s")
-            weave_u(0, 0, "v")
-            load_x(2)
-            empty_f0(1, 1, "s")
-            load_w(5)
-            weave_u(1, 1, "s")
-            load_f0(2)
-            turn_f0(1, 0)
-            turn_w(0, 1)
-            quant_u(1)
-            empty_w(0, 1, "s")
-            empty_f0(1, 0, "s")
-            weave_u(0, 1, "s")
-            load_w(4)
-            gain(2)
-            load_w(7)
-            turn_w(1, 0)
-            gain_mm(3, 3)
-            turn_f0(2, 0)
-            load_w(6)
-            gain_out(3, 3, "s")
-            empty_w(1, 0, "s")
-            empty_f0(2, 0, "s")
-            widen(3, 1)
-            turn_f0(3, 1)
+            diag_x(1, "v")
+            diag_x(0, "v")
+            load_x(0)
+            diag_x(3, "v")
+            load_late()
+            spread(1)
             load_w(2)
-            quant_w(0)
-            turn_f0(3, 0)
-            empty_f0(3, 0, "s")
-            empty_f0(3, 1, "s")
-            load_f0(0)
-            quant_u(0)
-            widen(1, 1)
-            widen(2, 1)
-            gain_mm(3, 2)
-            weave_u(2, 1, "v")
-            gain_out(3, 2, "s")
-            turn_w(3, 1)
-            turn_f0(2, 1)
-            turn_w(1, 1)
-            empty_w(3, 1, "s")
-            load_pair(0)
-            empty_f0(2, 1, "s")
-            empty_w(1, 1, "s")
-            gain_mm(3, 0)
-            turn_w(2, 1)
-            load_f1(3)
-            load_pair(1)
-            empty_w(2, 1, "s")
+            gain(0)
+            load_x(1)
+            load_x(3)
+            load_w(0)
+            spread(0)
+            spread(2)
+            weave_u(0, 1, "s")
+            load_x(2)
             gain_mm(3, 1)
-            widen(7, 0)
-            turn_f0(0, 0)
-            turn_w(3, 0)
-            widen(7, 1)
-            gain_out(3, 0, "s")
-            turn_w(7, 0)
-            pair(0)
+            spread_out(2, "s")
+            load_f0(2)
+            spread_out(1, "v")
+            weave_u(0, 0, "v")
+            gain(1)
+            quant_u(0)
+            spread_out(0, "s")
+            load_f0(0)
+            weave_u(1, 0, "s")
             gain_out(3, 1, "s")
-            pair(3)
-            empty_f0(0, 0, "s")
-            turn_f0(0, 1)
-            quant_w(1)
-            weave_u(2, 0, "s")
+            gain_mm(3, 0)
+            gain_mm(3, 2)
+            gain_out(3, 0, "s")
+            widen(0, 1, 2)
+            turn_f0(2, 0)
             widen(2, 0)
+            halve_gains()
+            diag_z(3, "v")
             turn_w(2, 0)
-            quant_u(3)
-            quant_u(2)
-            empty_w(3, 0, "s")
-            gelu_table()
-            diag_z(1, "s")
-            quant_w(3)
-            mul_m(0)
-            widen(6, 0)
-            turn_w(7, 1)
-            gelu(0)
-            empty_f0(0, 1, "s")
-            widen(6, 1)
-            mul_m(1)
-            empty_w(7, 0, "s")
-            mul_m(3)
+            weave_u(1, 1, "s")
+            widen(2, 1)
+            turn_w(2, 1)
             empty_w(2, 0, "s")
-            widen(4, 0)
-            load_f1(2)
-            turn_w(6, 1)
-            empty_w(7, 1, "s")
-            load_f1(1)
-            turn_w(6, 0)
-            empty_w(6, 1, "s")
-            widen(5, 1)
-            empty_w(6, 0, "s")
-            turn_w(4, 0)
-            turn_f1(2)
-            gelu(1)
-            turn_w(5, 1)
-            turn_f1(3)
-            quant_w(2)
-            mul_m(2)
-            diag_z(6, "s")
-            diag_z(7, "s")
-            widen(5, 0)
-            empty_w(4, 0, "s")
-            widen(4, 1)
-            empty_f1(2, "s")
+            turn_f0(0, 1)
+            empty_f0(2, 0, "s")
+            load_w(3)
+            gain_out(3, 2, "s")
+            empty_f0(0, 1, "s")
+            gain(2)
+            gain_mm(3, 3)
+            widen(0, 0, 2)
+            widen(3, 1)
+            turn_w(0, 0)
+            load_w(1)
+            turn_w(0, 1)
+            load_f0(3)
+            load_f1(3)
+            empty_w(2, 1, "s")
+            load_w(4)
+            load_pair(0)
+            empty_w(0, 1, "s")
+            empty_w(0, 0, "s")
+            turn_f0(3, 0)
             diag_z(2, "s")
-            turn_w(4, 1)
-            quant_w(7)
-            turn_w(5, 0)
-            gelu(3)
-            mix(0)
-            empty_w(5, 0, "s")
-            mix(3)
-            mul_m(7)
-            quant_f0(2)
-            quant_w(6)
-            empty_w(5, 1, "s")
-            pair(1)
-            pair(2)
-            gelu(2)
-            quant_f0(0)
-            mul_m(6)
-            mix(1)
-            quant_w(5)
-            diag_z(5, "s")
-            mix(2)
-            empty_w(4, 1, "s")
-            gelu(7)
-            pair(6)
-            quant_w(4)
-            gelu(6)
-            mix(6)
-            weave_y(0, 0, "s")
-            quant_f0(3)
-            mul_m(5)
-            pair(7)
-            mix(7)
-            gelu(5)
-            pair(5)
-            mix(5)
-            weave_y(0, 1, "s")
-            diag_z(4, "s")
-            weave_y(0, 3, "s")
-            mul_m(4)
-            gelu(4)
-            quant_f1(2)
-            quant_f1(0)
-            pair(4)
-            mul_h0(3)
-            mix(4)
-            weave_y(0, 2, "s")
-            weave_y(1, 2, "v")
-            keep_h0(3)
-            weave_y(1, 1, "s")
-            weave_y(1, 3, "v")
-            weave_y(1, 0, "v")
-            mul_h0(0)
-            keep_h0(0)
+            widen(3, 0)
+            load_f1(0)
+            empty_f0(3, 0, "s")
+            turn_w(3, 1)
+            empty_w(3, 1, "s")
+            turn_f1(3)
             empty_f1(3, "s")
-            mul_h0(2)
-            quant_y(0)
-            quant_y(1)
-            keep_h0(2)
-            mul_h1(0)
-            quant_f0(1)
-            blend(0)
-            quant_f1(3)
+            turn_f0(0, 0)
+            load_f0(1)
+            quant_w(2)
+            turn_w(3, 0)
+            empty_f0(0, 0, "s")
+            empty_w(3, 0, "s")
+            load_w(7)
+            quant_u(1)
+            turn_f0(2, 1)
+            widen(1, 0)
+            turn_w(1, 0)
+            pair(2)
+            widen(1, 1)
+            empty_f0(2, 1, "s")
+            turn_f0(1, 1)
+            quant_w(3)
+            widen(4, 0)
+            turn_w(1, 1)
+            weave_u(2, 1, "v")
+            turn_f1(0)
+            empty_w(1, 0, "s")
+            gain_out(3, 3, "s")
+            weave_u(2, 0, "s")
+            empty_w(1, 1, "s")
+            load_w(5)
+            diag_z(6, "s")
+            quant_u(3)
+            turn_f0(3, 1)
+            quant_u(2)
+            quant_w(0)
+            pair(3)
+            empty_f0(3, 1, "s")
+            mul_m(3)
+            load_w(6)
+            gelu(3)
+            diag_z(0, "s")
+            quant_w(1)
+            load_pair(1)
+            mul_m(2)
+            widen(7, 0)
+            gelu(2)
+            mul_m(0)
+            mul_m(1)
+            empty_f0(1, 1, "s")
+            gelu(0)
+            widen(7, 1)
+            widen(4, 1)
+            diag_z(1, "s")
+            empty_f1(0, "s")
+            turn_w(4, 0)
+            empty_w(4, 0, "s")
+            load_f1(1)
+            turn_w(7, 1)
+            widen(5, 1)
+            diag_z(7, "s")
+            diag_z(5, "s")
+            turn_w(4, 1)
+            empty_w(7, 1, "s")
+            turn_f0(1, 0)
+            widen(5, 0)
+            empty_w(4, 1, "s")
+            turn_w(5, 1)
+            mix(2)
+            turn_w(7, 0)
+            empty_w(5, 1, "s")
+            mix(3)
+            gelu(1)
+            quant_w(4)
+            turn_w(5, 0)
+            pair(1)
+            diag_z(4, "s")
+            pair(0)
+            empty_f0(1, 0, "s")
+            empty_w(7, 0, "s")
+            widen(6, 0)
+            mul_m(4)
+            widen(6, 1)
             turn_f1(1)
+            quant_w(7)
+            mix(0)
+            turn_w(6, 0)
+            turn_w(6, 1)
+            mul_m(7)
+            weights()
+            empty_w(5, 0, "s")
+            quant_w(5)
+            gelu(4)
+            mul_m(5)
+            empty_w(6, 1, "s")
+            mix(1)
+            empty_w(6, 0, "s")
+            quant_f0(3)
+            quant_w(6)
+            gelu(7)
+            weave_y(0, 2, "s")
+            quant_f0(2)
+            weave_y(0, 1, "s")
+            quant_f1(3)
+            pair(4)
+            pair(7)
+            mix(4)
+            weave_y(0, 3, "s")
+            gelu(5)
+            mix(7)
+            mul_m(6)
+            pair(5)
+            quant_f0(0)
+            gelu(6)
+            load_f1(2)
+            mix(5)
+            weave_y(0, 0, "s")
+            pair(6)
+            mix(6)
+            weave_y(1, 3, "v")
+            turn_f1(2)
+            mul_h0(0)
+            weave_y(1, 0, "v")
+            weave_y(1, 1, "s")
+            mul_h0(3)
+            quant_y(0)
+            weave_y(1, 2, "s")
+            quant_y(1)
+            quant_f0(1)
+            quant_f1(0)
+            keep_h0(0)
+            keep_h0(3)
+            mul_h1(3)
+            empty_f1(2, "s")
             empty_f1(1, "s")
-            quant_f1(1)
+            blend(3)
+            mul_h0(2)
+            quant_f1(2)
             mul_h0(1)
+            keep_h0(2)
+            quant_f1(1)
             keep_h0(1)
+            mul_h1(0)
+            mul_h1(1)
+            blend(0)
+            blend(1, 2)
             mul_h1(2)
             blend(2)
-            mul_h1(3)
-            blend(3)
-            mul_h1(1)
-            blend(1)

@@ -13,58 +13,102 @@ ACT = mybir.ActivationFunctionType
 ALU = mybir.AluOpType
 
 P = 128
-B, S, D, HZ = 2, 2048, 256, 512
-S1 = S // 2
-COLS = B * D
-PASSES = S // 512
-CPASSES = S1 // 512
-FLOPS = 2 * COLS * (S1 * S + HZ * S + HZ * S1)
-BYTES = 2 * (B * S * D + S + S1 + HZ * S + HZ * S1 + HZ) + S1 * S + 4 * S + 4 * B * HZ * D
+PACK = 4
+K_PASS = P * PACK
+BATCH, FINE, FEATURES, HORIZON = 2, 2048, 256, 512
+COARSE = FINE // 2
+COLS = BATCH * FEATURES
+FINE_PASSES = FINE // K_PASS
+COARSE_PASSES = COARSE // K_PASS
+MIX_TILES = COARSE // P
+OUT_TILES = HORIZON // P
+
+PE_GAIN_PASS = 3
+PASS_ORDER = (0, 3, 1, 2)
+FLOPS = 2 * COLS * (COARSE * FINE + HORIZON * FINE + HORIZON * COARSE)
 
 
 def tile_timemixerpyramidforecast_kernel(tc, x, g0, w01_bytes, w01_scale, g1, f0, f1, ens, out):
     nc = tc.nc
     with ExitStack() as ctx:
         keep = ctx.enter_context(tc.tile_pool(name="keep", bufs=1))
-        work = ctx.enter_context(tc.tile_pool(name="work", bufs=3))
-        psum = ctx.enter_context(tc.psum_pool(name="psum", bufs=1))
+        work = ctx.enter_context(tc.tile_pool(name="work", bufs=2))
+        psum = ctx.enter_context(tc.psum_pool(name="psum", bufs=2))
 
-        def kt(shape, dtype, name):
+        def kept(name, shape, dtype):
             return keep.tile(shape, dtype, name=name, align_bytes=64)
 
-        s_rows = kt([P, P], F32, "s_rows")
-        g0_col = kt([P, PASSES, 4], BF16, "g0_col")
-        g1_col = kt([P, CPASSES, 4], BF16, "g1_col")
-        ens_col = kt([P, 4], BF16, "ens_col")
-        nc.gpsimd.memset(s_rows[:], 0.0)
+        scale_rows = kept("scale_rows", [P, P], F32)
+        scale_cols = kept("scale_cols", [P, 16], F32)
+        scale = kept("scale", [P, FINE], F32)
+        g0_col = kept("g0_col", [P, FINE_PASSES, 16], BF16)
+        g1_col = kept("g1_col", [P, COARSE_PASSES, PACK], BF16)
+        g1_half = kept("g1_half", [P, COARSE_PASSES, PACK], F32)
+        ens_col = kept("ens_col", [P, OUT_TILES], BF16)
+        tanh_col = kept("tanh_col", [P, OUT_TILES], F32)
+        a_col = kept("a_col", [P, OUT_TILES], F32)
+        rest_col = kept("rest_col", [P, OUT_TILES], F32)
+        zero = kept("zero", [P, 1], F32)
+        table_out = kept("table_out", [P, 1], F32)
+        ident = kept("ident", [P, P], F32)
+        ident_bf = kept("ident_bf", [P, P], BF16)
+        gain_diag = kept("gain_diag", [P, PACK, P], BF16)
+        pair_diag = [kept(f"pair_diag{j}", [P, P], BF16) for j in range(MIX_TILES)]
 
-        scale = kt([P, S], F32, "scale")
-        w_raw = [kt([P, S], U8, f"w_raw{j}") for j in range(8)]
-        x_fine = [kt([P, B, 4 * D], BF16, f"x_fine{g}") for g in range(PASSES)]
-        x_pair = [kt([P, B, 8 * D], BF16, f"x_pair{g}") for g in range(CPASSES)]
-        f0_raw = [kt([P, S], BF16, f"f0_raw{i}") for i in range(4)]
-        f1_raw = [kt([P, S1], BF16, f"f1_raw{i}") for i in range(4)]
+        w_raw = [kept(f"w_raw{j}", [P, FINE], U8) for j in range(MIX_TILES)]
+        x_fine = [kept(f"x_fine{g}", [P, BATCH, PACK * FEATURES], BF16) for g in range(FINE_PASSES)]
+        x_pair = [kept(f"x_pair{g}", [P, BATCH, 2 * PACK * FEATURES], BF16) for g in range(COARSE_PASSES)]
+        f0_raw = [kept(f"f0_raw{i}", [P, FINE], BF16) for i in range(OUT_TILES)]
+        f1_raw = [kept(f"f1_raw{i}", [P, COARSE], BF16) for i in range(OUT_TILES)]
 
-        w_rows = w01_bytes.rearrange("(g m t) k -> g t m k", g=2, t=4)
-        f0_rows = f0.rearrange("(m t) k -> t m k", t=4)
-        f1_rows = f1.rearrange("(m t) k -> t m k", t=4)
+        def operand(name, words):
+            return kept(name + "_codes", [P, words], U32), kept(name + "_scales", [P, words], U8)
 
-        def load_consts():
-            nc.sync.dma_start(out=s_rows[0:16, :], in_=w01_scale.rearrange("o (m n) -> (o m) n", n=P))
-            nc.sync.dma_start(out=g0_col[:], in_=g0.rearrange("(g p t) -> p g t", p=P, t=4))
+        u_mx = [operand(f"u{g}", COLS) for g in range(FINE_PASSES)]
+        y_mx = [operand(f"y{g}", COLS) for g in range(COARSE_PASSES)]
+        w_mx = [operand(f"w{j}", FINE // PACK) for j in range(MIX_TILES)]
+        f0_mx = [operand(f"f0_{i}", FINE // PACK) for i in range(OUT_TILES)]
+        f1_mx = [operand(f"f1_{i}", COARSE // PACK) for i in range(OUT_TILES)]
+        y_planes = [kept(f"y_planes{g}", [P, PACK, COLS], BF16) for g in range(COARSE_PASSES)]
+        h0_part = [kept(f"h0_part{i}", [P, COLS], F32) for i in range(OUT_TILES)]
 
-        def load_late():
-            nc.sync.dma_start(out=g1_col[:], in_=g1.rearrange("(g p t) -> p g t", p=P, t=4))
-            nc.sync.dma_start(out=ens_col[:], in_=ens.rearrange("(m t) -> m t", t=4))
+        live = {}
+        depth = {"w_bf": 3, "w_g": 3, "f0_g": 4, "f1_g": 2, "x_s": 2, "u_g": 2, "gelu": 3, "y_g": 2, "o": 3, "tp": 4, "m": 2, "acc": 2}
+
+        def made(tag, n, shape, dtype):
+            if (tag, n) not in live:
+                live[tag, n] = work.tile(shape, dtype, name=tag, bufs=depth[tag], align_bytes=64)
+            return live[tag, n]
+
+        def bank(tag, key, shape):
+            live[key] = psum.tile(shape, F32, name=tag, bufs=depth[tag])
+            return live[key]
+
+        w_rows = w01_bytes.rearrange("(g m t) k -> g t m k", g=COARSE_PASSES, t=PACK)
+        f0_rows = f0.rearrange("(m t) k -> t m k", t=PACK)
+        f1_rows = f1.rearrange("(m t) k -> t m k", t=PACK)
+        out_rows = out.rearrange("b (m t) n -> t m b n", t=PACK)
+
+        def load_scales():
+            nc.sync.dma_start(out=scale_rows[0:16, :], in_=w01_scale.rearrange("o (r n) -> (o r) n", n=P))
+
+        def load_g0(g):
+            nc.sync.dma_start(out=g0_col[:, g, 0:PACK], in_=g0[g * K_PASS : (g + 1) * K_PASS].rearrange("(p t) -> p t", t=PACK))
+
+        def load_g1_ens():
+            nc.sync.dma_start(out=g1_col[:], in_=g1.rearrange("(g p t) -> p g t", p=P, t=PACK))
+            nc.sync.dma_start(out=ens_col[:], in_=ens.rearrange("(m t) -> m t", t=PACK))
 
         def load_w(j):
-            nc.sync.dma_start(out=w_raw[j][:], in_=w_rows[j // 4, j % 4])
+            nc.sync.dma_start(out=w_raw[j][:], in_=w_rows[j // PACK, j % PACK])
 
         def load_x(g):
-            nc.sync.dma_start(out=x_fine[g][:], in_=x[:, g * 512 : (g + 1) * 512, :].rearrange("b (p t) n -> p b (t n)", t=4))
+            for b in range(BATCH):
+                nc.sync.dma_start(out=x_fine[g][:, b, :], in_=x[b, g * K_PASS : (g + 1) * K_PASS, :].rearrange("(p t) n -> p (t n)", t=PACK))
 
         def load_pair(g):
-            nc.sync.dma_start(out=x_pair[g][:], in_=x[:, g * 1024 : (g + 1) * 1024, :].rearrange("b (p t) n -> p b (t n)", t=8))
+            steps = slice(2 * g * K_PASS, 2 * (g + 1) * K_PASS)
+            nc.sync.dma_start(out=x_pair[g][:], in_=x[:, steps, :].rearrange("b (p s) n -> p b (s n)", s=2 * PACK))
 
         def load_f0(i):
             nc.sync.dma_start(out=f0_raw[i][:], in_=f0_rows[i])
@@ -72,465 +116,388 @@ def tile_timemixerpyramidforecast_kernel(tc, x, g0, w01_bytes, w01_scale, g1, f0
         def load_f1(i):
             nc.sync.dma_start(out=f1_raw[i][:], in_=f1_rows[i])
 
-
-        a_col = kt([P, 4], F32, "a_col")
-        na_col = kt([P, 4], F32, "na_col")
-        dummy = kt([P, 1], F32, "dummy")
-        zero = kt([P, 1], F32, "zero")
-        nc.vector.memset(zero[:], 0.0)
-        nc.scalar.activation(out=dummy[:], in_=zero[:], func=ACT.Gelu_apprx_tanh)
-        ident = kt([P, P], F32, "ident")
-        make_identity(nc, ident[:])
-        ident_b = kt([P, P], BF16, "ident_b")
-        nc.gpsimd.tensor_copy(out=ident_b[:], in_=ident[:])
-        s_cols = kt([P, 16], F32, "s_cols")
-        th_col = kt([P, 4], F32, "th_col")
-        g1_half = kt([P, CPASSES, 4], F32, "g1_half")
-        d0 = kt([P, 4, P], BF16, "d0")
-        dz = [kt([P, 4, P], BF16, f"dz{g}") for g in range(CPASSES)]
-
-        u_codes = [kt([P, COLS], U32, f"u_codes{g}") for g in range(PASSES)]
-        u_sc = [kt([P, COLS], U8, f"u_sc{g}") for g in range(PASSES)]
-        w_codes = [kt([P, PASSES * P], U32, f"w_codes{j}") for j in range(8)]
-        w_sc = [kt([P, PASSES * P], U8, f"w_sc{j}") for j in range(8)]
-        f0_codes = [kt([P, PASSES * P], U32, f"f0_codes{i}") for i in range(4)]
-        f0_sc = [kt([P, PASSES * P], U8, f"f0_sc{i}") for i in range(4)]
-        f1_codes = [kt([P, CPASSES * P], U32, f"f1_codes{i}") for i in range(4)]
-        f1_sc = [kt([P, CPASSES * P], U8, f"f1_sc{i}") for i in range(4)]
-        y_codes = [kt([P, COLS], U32, f"y_codes{g}") for g in range(CPASSES)]
-        y_sc = [kt([P, COLS], U8, f"y_sc{g}") for g in range(CPASSES)]
-        yp = [kt([P, 4, COLS], BF16, f"yp{g}") for g in range(CPASSES)]
-        h0_part = [kt([P, COLS], F32, f"h0_part{i}") for i in range(4)]
-        live = {}
-
-        depth = {"w_bf": 3, "w_g": 3, "f0_g": 4, "f1_g": 2, "u_g": 2, "y_g": 2}
-
-        def shared(name, n, width):
-            if (name, n) not in live:
-                live[name, n] = work.tile([P, width], BF16, name=name, bufs=depth[name], align_bytes=64)
-            return live[name, n]
-
-        def tp_bank():
-            return psum.tile([P, 2, 2, P], F32, name="tp", bufs=4)
-
-        def turn_consts():
-            bank = tp_bank()
-            live["consts"] = bank
-            nc.tensor.transpose(bank[:, 0, 0, :], s_rows[:], ident[:])
+        def turn_scales():
+            nc.tensor.transpose(bank("tp", ("scales", 0), [P, P])[:], scale_rows[:], ident[:])
 
         def fetch_scales():
-            nc.scalar.copy(out=s_cols[:], in_=live["consts"][:, 0, 0, 0:16])
-
-        def halve_gains():
-            nc.gpsimd.tensor_scalar(out=g1_half[:], in0=g1_col[:], scalar1=0.5, scalar2=0.0, op0=ALU.mult, op1=ALU.add)
-
-        def weights():
-            nc.scalar.activation(out=th_col[:], in_=ens_col[:], func=ACT.Tanh, scale=0.5)
-            nc.gpsimd.tensor_scalar(out=a_col[:], in0=th_col[:], scalar1=0.5, scalar2=0.5, op0=ALU.mult, op1=ALU.add)
-            nc.gpsimd.tensor_scalar(out=na_col[:], in0=th_col[:], scalar1=-0.5, scalar2=0.5, op0=ALU.mult, op1=ALU.add)
+            nc.scalar.copy(out=scale_cols[:], in_=live["scales", 0][:, 0:16])
 
         def spread(q):
-            bank = tp_bank()
-            live["spread", q] = bank
+            spot = bank("tp", ("spread", q), [P, 4, P])
             for i in range(4):
-                nc.tensor.transpose(bank[:, i // 2, i % 2, :], s_cols[:, 4 * q + i : 4 * q + i + 1].to_broadcast([P, P]), ident[:])
+                r = 4 * q + i
+                nc.tensor.transpose(spot[:, i, :], scale_cols[:, r : r + 1].to_broadcast([P, P]), ident[:])
 
-        def spread_out(q, eng="s"):
-            o = scale[:, 512 * q : 512 * (q + 1)]
-            i = live["spread", q][:].rearrange("p g u n -> p (g u n)")
-            if eng == "s":
-                nc.scalar.copy(out=o, in_=i)
-            else:
-                nc.vector.tensor_copy(out=o, in_=i)
+        def spread_out(q, eng):
+            copy_of(eng)(out=scale[:, q * 512 : (q + 1) * 512], in_=live["spread", q][:].rearrange("p r n -> p (r n)"))
 
-        def diag(dst, t, col, eng):
-            if eng == "s":
-                nc.scalar.activation(out=dst[:, t, :], in_=ident_b[:], func=ACT.Copy, scale=col)
-            else:
-                nc.vector.tensor_scalar(out=dst[:, t, :], in0=ident_b[:], scalar1=col, scalar2=None, op0=ALU.mult)
+        def copy_of(eng):
+            return nc.scalar.copy if eng == "s" else nc.vector.tensor_copy
 
-        def diag_x(t, eng="v"):
-            diag(d0, t, g0_col[:, 3, t : t + 1], eng)
-
-        def diag_z(j, eng="v"):
-            diag(dz[j // 4], j % 4, g1_half[:, j // 4, j % 4 : j % 4 + 1], eng)
-
-        def widen(j, h, chunks=1):
-            t = shared("w_bf", j, S)
-            n = S // 2 // chunks
-            for c in range(chunks):
-                cols = slice(h * (S // 2) + c * n, h * (S // 2) + (c + 1) * n)
-                nc.vector.tensor_tensor(out=t[:, cols], in0=w_raw[j][:, cols].bitcast(FP8), in1=scale[:, cols], op=ALU.mult)
-
-        def turn(src, half):
+        def turn(src, half, key):
             words = src[:].bitcast(F32)
-            bank = tp_bank()
-            for gg in range(2):
-                for u in range(2):
-                    lo = 256 * (2 * half + gg)
-                    nc.tensor.transpose(bank[:, gg, u, :], words[:, lo + u : lo + 256 : 2], ident[:])
-            return bank
+            spot = bank("tp", key, [P, 2, 2, P])
+            for g in range(2):
+                lo = (2 * half + g) * K_PASS // 2
+                for e in range(2):
+                    nc.tensor.transpose(spot[:, g, e, :], words[:, lo + e : lo + K_PASS // 2 : 2], ident[:])
 
-        def empty(dst, half, bank, eng):
-            o = dst[:, half * 1024 : (half + 1) * 1024].bitcast(F32).rearrange("p (g r u) -> p g r u", g=2, u=2)
-            i = bank[:].rearrange("p g u r -> p g r u")
-            if eng == "s":
-                nc.scalar.copy(out=o, in_=i)
-            else:
-                nc.vector.tensor_copy(out=o, in_=i)
+        def empty(dst, half, key):
+            n = 2 * K_PASS
+            nc.scalar.copy(
+                out=dst[:, half * n : (half + 1) * n].bitcast(F32).rearrange("p (g r e) -> p g r e", g=2, e=2),
+                in_=live[key][:].rearrange("p g e r -> p g r e"),
+            )
 
+        def quantise(operand_tiles, src):
+            codes, scales = operand_tiles
+            nc.vector.quantize_mx(out=codes[:].bitcast(FP8X4), scales=scales[:], in_=src[:])
 
-        def turn_w(j, h):
-            live["wt", j, h] = turn(live["w_bf", j], h)
+        def widen(j, chunks=1):
+            dst = made("w_bf", j, [P, FINE], BF16)
+            n = FINE // chunks
+            for c in range(chunks):
+                cols = slice(c * n, (c + 1) * n)
+                nc.vector.tensor_tensor(out=dst[:, cols], in0=w_raw[j][:, cols].bitcast(FP8), in1=scale[:, cols], op=ALU.mult)
 
-        def empty_w(j, h, eng="s"):
-            empty(shared("w_g", j, S), h, live["wt", j, h], eng)
+        def turn_w(j):
+            for half in range(2):
+                turn(live["w_bf", j], half, ("w_turned", j, half))
+
+        def empty_w(j):
+            for half in range(2):
+                empty(made("w_g", j, [P, FINE], BF16), half, ("w_turned", j, half))
 
         def quant_w(j):
-            nc.vector.quantize_mx(out=w_codes[j][:].bitcast(FP8X4), scales=w_sc[j][:], in_=live["w_g", j][:])
+            quantise(w_mx[j], live["w_g", j])
 
-        def turn_f0(i, h):
-            live["f0t", i, h] = turn(f0_raw[i], h)
+        def turn_f0(i):
+            for half in range(2):
+                turn(f0_raw[i], half, ("f0_turned", i, half))
 
-        def empty_f0(i, h, eng="s"):
-            empty(shared("f0_g", i, S), h, live["f0t", i, h], eng)
+        def empty_f0(i):
+            for half in range(2):
+                empty(made("f0_g", i, [P, FINE], BF16), half, ("f0_turned", i, half))
 
         def quant_f0(i):
-            nc.vector.quantize_mx(out=f0_codes[i][:].bitcast(FP8X4), scales=f0_sc[i][:], in_=live["f0_g", i][:])
+            quantise(f0_mx[i], live["f0_g", i])
 
         def turn_f1(i):
-            live["f1t", i] = turn(f1_raw[i], 0)
+            turn(f1_raw[i], 0, ("f1_turned", i))
 
-        def empty_f1(i, eng="s"):
-            empty(shared("f1_g", i, S1), 0, live["f1t", i], eng)
+        def empty_f1(i):
+            empty(made("f1_g", i, [P, COARSE], BF16), 0, ("f1_turned", i))
 
         def quant_f1(i):
-            nc.vector.quantize_mx(out=f1_codes[i][:].bitcast(FP8X4), scales=f1_sc[i][:], in_=live["f1_g", i][:])
+            quantise(f1_mx[i], live["f1_g", i])
 
         def gain(g):
-            t = work.tile([P, 4, COLS], BF16, name="x_s", bufs=2, align_bytes=64)
-            live["xs", g] = t
-            for k in range(4):
+            dst = made("x_s", g, [P, PACK, COLS], BF16)
+            for t in range(PACK):
                 nc.vector.tensor_scalar(
-                    out=t[:, k, :].rearrange("p (b n) -> p b n", b=B),
-                    in0=x_fine[g][:, :, k * D : (k + 1) * D],
-                    scalar1=g0_col[:, g, k : k + 1],
+                    out=dst[:, t, :].rearrange("p (b n) -> p b n", b=BATCH),
+                    in0=x_fine[g][:, :, t * FEATURES : (t + 1) * FEATURES],
+                    scalar1=g0_col[:, g, t : t + 1],
                     scalar2=None,
                     op0=ALU.mult,
                 )
 
-        def weave(dst, src, eng, c0=0, c1=COLS):
-            o = dst[:].rearrange("p (c t) -> p c t", t=4)[:, c0:c1, :]
-            i = src[:].rearrange("p t c -> p c t")[:, c0:c1, :]
-            if eng == "s":
-                nc.scalar.copy(out=o, in_=i)
-            else:
-                nc.vector.tensor_copy(out=o, in_=i)
+        def weave(dst, src, c0, c1, eng):
+            copy_of(eng)(
+                out=dst[:, PACK * c0 : PACK * c1].rearrange("p (c i t) -> p c t i", i=4, t=PACK),
+                in_=src[:, :, c0:c1].rearrange("p t (c i) -> p c t i", i=4),
+            )
 
-        def weave_u(g, h, eng="s"):
-            weave(shared("u_g", g, 4 * COLS), live["xs", g], eng, h * D, (h + 1) * D)
+        def weave_u(g, b, eng):
+            weave(made("u_g", g, [P, PACK * COLS], BF16), live["x_s", g], b * FEATURES, (b + 1) * FEATURES, eng)
 
-        def gain_mm(g, c):
-            bank = psum.tile([P, 4, P], F32, name="zh", bufs=2)
-            live["gb", g, c] = bank
-            b, n0 = c // 2, (c % 2) * P
-            for k in range(4):
-                nc.tensor.matmul(bank[:, k, :], lhsT=d0[:, k, :], rhs=x_fine[g][:, b, k * D + n0 : k * D + n0 + P], start=True, stop=True)
+        def make_gain_diag():
+            for t in range(PACK):
+                nc.vector.tensor_scalar(out=gain_diag[:, t, :], in0=ident_bf[:], scalar1=g0_col[:, PE_GAIN_PASS, t : t + 1], scalar2=None, op0=ALU.mult)
 
-        def gain_out(g, c, eng="s"):
-            o = shared("u_g", g, 4 * COLS)[:, c * 512 : (c + 1) * 512].rearrange("p (n t) -> p n t", t=4)
-            i = live["gb", g, c][:].rearrange("p t n -> p n t")
-            if eng == "s":
-                nc.scalar.copy(out=o, in_=i)
-            else:
-                nc.vector.tensor_copy(out=o, in_=i)
+        def gain_mm(q):
+            g, b, n0 = PE_GAIN_PASS, q // 2, (q % 2) * P
+            spot = bank("acc", ("gained", q), [P, PACK, P])
+            for t in range(PACK):
+                lo = t * FEATURES + n0
+                nc.tensor.matmul(spot[:, t, :], lhsT=gain_diag[:, t, :], rhs=x_fine[g][:, b, lo : lo + P], start=True, stop=True)
+
+        def gain_out(q):
+            nc.scalar.copy(
+                out=made("u_g", PE_GAIN_PASS, [P, PACK * COLS], BF16)[:, q * K_PASS : (q + 1) * K_PASS].rearrange("p (n t) -> p n t", t=PACK),
+                in_=live["gained", q][:].rearrange("p t n -> p n t"),
+            )
 
         def quant_u(g):
-            nc.vector.quantize_mx(out=u_codes[g][:].bitcast(FP8X4), scales=u_sc[g][:], in_=live["u_g", g][:])
+            quantise(u_mx[g], live["u_g", g])
 
-        def mx(acc, codes, sc, mov, mov_sc, passes):
-            for g in range(passes):
+        def multiply(tag, key, stationary, moving, passes):
+            acc = bank(tag, key, [P, COLS])
+            codes, scales = stationary
+            for g in passes:
+                rows = slice(g * P, (g + 1) * P)
                 nc.tensor.matmul_mx(
                     out=acc[:],
-                    lhsT=codes[:, g * P : (g + 1) * P].bitcast(FP8X4),
-                    lhsT_scale=sc[:, g * P : (g + 1) * P],
-                    rhs=mov[g][:].bitcast(FP8X4),
-                    rhs_scale=mov_sc[g][:],
-                    start=(g == 0),
-                    stop=(g == passes - 1),
+                    lhsT=codes[:, rows].bitcast(FP8X4),
+                    lhsT_scale=scales[:, rows],
+                    rhs=moving[g][0][:].bitcast(FP8X4),
+                    rhs_scale=moving[g][1][:],
+                    start=(g == passes[0]),
+                    stop=(g == passes[-1]),
                 )
 
         def mul_m(j):
-            acc = psum.tile([P, COLS], F32, name="m", bufs=2)
-            live["m", j] = acc
-            mx(acc, w_codes[j], w_sc[j], u_codes, u_sc, PASSES)
-
-        def gelu(j):
-            t = work.tile([P, COLS], F32, name="ge")
-            live["ge", j] = t
-            nc.scalar.activation(out=t[:], in_=live["m", j][:], func=ACT.Gelu_apprx_tanh)
-
-        def pair(j):
-            g, k = j // 4, j % 4
-            acc = psum.tile([P, COLS], F32, name="zh", bufs=2)
-            live["z", j] = acc
-            for e in range(2):
-                s = 2 * k + e
-                nc.tensor.matmul(acc[:].rearrange("p (b n) -> p b n", b=B), lhsT=dz[g][:, k, :], rhs=x_pair[g][:, :, s * D : (s + 1) * D], start=(e == 0), stop=(e == 1))
-
-        def mix(j):
-            g, k = j // 4, j % 4
-            nc.vector.scalar_tensor_tensor(out=yp[g][:, k, :], in0=live["ge", j][:], scalar=g1_col[:, g, k : k + 1], in1=live["z", j][:], op0=ALU.mult, op1=ALU.add)
-
-        def weave_y(g, q, eng):
-            weave(shared("y_g", g, 4 * COLS), yp[g], eng, q * P, (q + 1) * P)
-
-        def quant_y(g):
-            nc.vector.quantize_mx(out=y_codes[g][:].bitcast(FP8X4), scales=y_sc[g][:], in_=live["y_g", g][:])
+            multiply("m", ("m", j), w_mx[j], u_mx, PASS_ORDER)
 
         def mul_h0(i):
-            acc = psum.tile([P, COLS], F32, name="zh", bufs=2)
-            live["h0", i] = acc
-            mx(acc, f0_codes[i], f0_sc[i], u_codes, u_sc, PASSES)
+            multiply("acc", ("h0", i), f0_mx[i], u_mx, PASS_ORDER)
+
+        def mul_h1(i):
+            multiply(("acc", "m", "m", "acc")[i], ("h1", i), f1_mx[i], y_mx, (0, 1))
+
+        def halve_gains():
+            nc.gpsimd.tensor_scalar(out=g1_half[:], in0=g1_col[:], scalar1=0.5, scalar2=0.0, op0=ALU.mult, op1=ALU.add)
+
+        def diag_z(j, eng):
+            col = g1_half[:, j // PACK, j % PACK : j % PACK + 1]
+            if eng == "s":
+                nc.scalar.activation(out=pair_diag[j][:], in_=ident_bf[:], func=ACT.Copy, scale=col)
+            else:
+                nc.vector.tensor_scalar(out=pair_diag[j][:], in0=ident_bf[:], scalar1=col, scalar2=None, op0=ALU.mult)
+
+        def pair(j):
+            acc = bank("acc", ("z", j), [P, COLS])
+            for e in range(2):
+                s = 2 * (j % PACK) + e
+                nc.tensor.matmul(
+                    acc[:].rearrange("p (b n) -> p b n", b=BATCH),
+                    lhsT=pair_diag[j][:],
+                    rhs=x_pair[j // PACK][:, :, s * FEATURES : (s + 1) * FEATURES],
+                    start=(e == 0),
+                    stop=(e == 1),
+                )
+
+        def gelu(j):
+            nc.scalar.activation(out=made("gelu", j, [P, COLS], F32)[:], in_=live["m", j][:], func=ACT.Gelu_apprx_tanh)
+
+        def mix(j):
+            g, t = j // PACK, j % PACK
+            nc.vector.scalar_tensor_tensor(
+                out=y_planes[g][:, t, :], in0=live["gelu", j][:], scalar=g1_col[:, g, t : t + 1], in1=live["z", j][:], op0=ALU.mult, op1=ALU.add
+            )
+
+        def weave_y(g, q, eng):
+            weave(made("y_g", g, [P, PACK * COLS], BF16), y_planes[g], q * P, (q + 1) * P, eng)
+
+        def quant_y(g):
+            quantise(y_mx[g], live["y_g", g])
+
+        def weights():
+            nc.scalar.activation(out=tanh_col[:], in_=ens_col[:], func=ACT.Tanh, scale=0.5)
+            nc.gpsimd.tensor_scalar(out=a_col[:], in0=tanh_col[:], scalar1=0.5, scalar2=0.5, op0=ALU.mult, op1=ALU.add)
+            nc.gpsimd.tensor_scalar(out=rest_col[:], in0=tanh_col[:], scalar1=-0.5, scalar2=0.5, op0=ALU.mult, op1=ALU.add)
 
         def keep_h0(i):
             nc.scalar.activation(out=h0_part[i][:], in_=live["h0", i][:], func=ACT.Copy, scale=a_col[:, i : i + 1])
 
-        def mul_h1(i):
-            acc = psum.tile([P, COLS], F32, name=("zh", "m")[i % 2], bufs=2)
-            live["h1", i] = acc
-            mx(acc, f1_codes[i], f1_sc[i], y_codes, y_sc, CPASSES)
-
-        out_rows = out.rearrange("b (m t) n -> t m b n", t=4)
-
         def blend(i, pieces=1):
-            o = work.tile([P, B, D], F32, name="o")
-            n = B // pieces
+            o = made("o", i, [P, COLS], F32)
+            n = BATCH // pieces
             for c in range(pieces):
-                cols_c = slice(c * n * D, (c + 1) * n * D)
+                cols = slice(c * n * FEATURES, (c + 1) * n * FEATURES)
                 nc.vector.scalar_tensor_tensor(
-                    out=o[:].rearrange("p b n -> p (b n)")[:, cols_c],
-                    in0=live["h1", i][:, cols_c],
-                    scalar=na_col[:, i : i + 1],
-                    in1=h0_part[i][:, cols_c],
-                    op0=ALU.mult,
-                    op1=ALU.add,
+                    out=o[:, cols], in0=live["h1", i][:, cols], scalar=rest_col[:, i : i + 1], in1=h0_part[i][:, cols], op0=ALU.mult, op1=ALU.add
                 )
-                nc.sync.dma_start(out=out_rows[i][:, c * n : (c + 1) * n, :], in_=o[:, c * n : (c + 1) * n, :])
+                nc.sync.dma_start(out=out_rows[i][:, c * n : (c + 1) * n, :], in_=o[:, cols].rearrange("p (b n) -> p b n", n=FEATURES))
 
-        with tc.manual_schedule(engines={mybir.EngineType.PE, mybir.EngineType.DVE, mybir.EngineType.Activation}):
-            load_consts()
-            turn_consts()
-            diag_x(2, "v")
-            fetch_scales()
-            spread(3)
-            spread_out(3, "s")
-            diag_x(1, "v")
-            diag_x(0, "v")
+        nc.gpsimd.memset(scale_rows[:], 0.0)
+        make_identity(nc, ident[:])
+        nc.gpsimd.tensor_copy(out=ident_bf[:], in_=ident[:])
+        nc.vector.memset(zero[:], 0.0)
+        nc.scalar.activation(out=table_out[:], in_=zero[:], func=ACT.Gelu_apprx_tanh)
+
+        with tc.manual_schedule():
+            load_scales()
             load_x(0)
-            diag_x(3, "v")
-            load_late()
-            spread(1)
-            load_w(2)
-            gain(0)
-            load_x(1)
-            load_x(3)
+            load_g0(0)
+            load_g0(3)
             load_w(0)
-            spread(0)
-            spread(2)
-            weave_u(0, 1, "s")
-            load_x(2)
-            gain_mm(3, 1)
-            spread_out(2, "s")
             load_f0(2)
-            spread_out(1, "v")
-            weave_u(0, 0, "v")
-            gain(1)
-            quant_u(0)
-            spread_out(0, "s")
-            load_f0(0)
-            weave_u(1, 0, "s")
-            gain_out(3, 1, "s")
-            gain_mm(3, 0)
-            gain_mm(3, 2)
-            gain_out(3, 0, "s")
-            widen(0, 1, 2)
-            turn_f0(2, 0)
-            widen(2, 0)
-            halve_gains()
-            diag_z(3, "v")
-            turn_w(2, 0)
-            weave_u(1, 1, "s")
-            widen(2, 1)
-            turn_w(2, 1)
-            empty_w(2, 0, "s")
-            turn_f0(0, 1)
-            empty_f0(2, 0, "s")
-            load_w(3)
-            gain_out(3, 2, "s")
-            empty_f0(0, 1, "s")
-            gain(2)
-            gain_mm(3, 3)
-            widen(0, 0, 2)
-            widen(3, 1)
-            turn_w(0, 0)
             load_w(1)
-            turn_w(0, 1)
+            load_x(3)
+            load_w(3)
+            load_w(2)
+            load_g0(1)
+            load_x(1)
+            load_f1(1)
             load_f0(3)
-            load_f1(3)
-            empty_w(2, 1, "s")
-            load_w(4)
-            load_pair(0)
-            empty_w(0, 1, "s")
-            empty_w(0, 0, "s")
-            turn_f0(3, 0)
-            diag_z(2, "s")
-            widen(3, 0)
+            load_g1_ens()
             load_f1(0)
-            empty_f0(3, 0, "s")
-            turn_w(3, 1)
-            empty_w(3, 1, "s")
-            turn_f1(3)
-            empty_f1(3, "s")
-            turn_f0(0, 0)
+            load_x(2)
+            load_w(4)
+            load_f0(0)
+            load_pair(0)
+            load_g0(2)
             load_f0(1)
-            quant_w(2)
-            turn_w(3, 0)
-            empty_f0(0, 0, "s")
-            empty_w(3, 0, "s")
             load_w(7)
-            quant_u(1)
-            turn_f0(2, 1)
-            widen(1, 0)
-            turn_w(1, 0)
-            pair(2)
-            widen(1, 1)
-            empty_f0(2, 1, "s")
-            turn_f0(1, 1)
-            quant_w(3)
-            widen(4, 0)
-            turn_w(1, 1)
-            weave_u(2, 1, "v")
-            turn_f1(0)
-            empty_w(1, 0, "s")
-            gain_out(3, 3, "s")
-            weave_u(2, 0, "s")
-            empty_w(1, 1, "s")
             load_w(5)
-            diag_z(6, "s")
-            quant_u(3)
-            turn_f0(3, 1)
-            quant_u(2)
-            quant_w(0)
-            pair(3)
-            empty_f0(3, 1, "s")
-            mul_m(3)
             load_w(6)
-            gelu(3)
-            diag_z(0, "s")
-            quant_w(1)
+            load_f1(3)
             load_pair(1)
+            load_f1(2)
+            turn_scales()
+            fetch_scales()
+            spread(0)
+            gain(0)
+            spread(1)
+            make_gain_diag()
+            spread_out(0, "s")
+            spread(2)
+            spread(3)
+            spread_out(1, "s")
+            spread_out(2, "s")
+            spread_out(3, "s")
+            widen(0, 4)
+            widen(1)
+            turn_w(0)
+            widen(2)
+            weave_u(0, 1, "s")
+            gain(1)
+            turn_f0(2)
+            gain_mm(2)
+            empty_w(0)
+            weave_u(0, 0, "s")
+            widen(3)
+            quant_w(0)
+            gain_mm(0)
+            empty_f0(2)
+            turn_w(1)
+            empty_w(1)
+            turn_f1(1)
+            empty_f1(1)
+            halve_gains()
+            gain_out(0)
+            diag_z(1, "v")
+            turn_w(2)
+            empty_w(2)
+            turn_f0(3)
+            diag_z(2, "v")
+            empty_f0(3)
+            gain_out(2)
+            quant_w(1)
+            turn_w(3)
+            turn_f1(0)
+            gain_mm(3)
+            empty_w(3)
+            quant_u(0)
+            gain_mm(1)
+            empty_f1(0)
+            widen(4)
+            weave_u(1, 1, "v")
+            turn_f0(0)
+            quant_w(2)
+            gain_out(1)
+            gain_out(3)
+            quant_u(3)
+            weave_u(1, 0, "s")
+            turn_w(4)
+            empty_f0(0)
+            gain(2)
+            weave_u(2, 0, "s")
+            quant_u(1)
+            weave_u(2, 1, "v")
+            pair(2)
+            quant_w(3)
+            diag_z(6, "s")
+            empty_w(4)
+            pair(1)
+            diag_z(3, "s")
+            diag_z(5, "s")
+            quant_u(2)
+            turn_f0(1)
+            mul_m(1)
+            gelu(1)
             mul_m(2)
-            widen(7, 0)
+            widen(5)
+            widen(6)
+            diag_z(0, "s")
+            mul_m(3)
             gelu(2)
             mul_m(0)
-            mul_m(1)
-            empty_f0(1, 1, "s")
-            gelu(0)
-            widen(7, 1)
-            widen(4, 1)
-            diag_z(1, "s")
-            empty_f1(0, "s")
-            turn_w(4, 0)
-            empty_w(4, 0, "s")
-            load_f1(1)
-            turn_w(7, 1)
-            widen(5, 1)
-            diag_z(7, "s")
-            diag_z(5, "s")
-            turn_w(4, 1)
-            empty_w(7, 1, "s")
-            turn_f0(1, 0)
-            widen(5, 0)
-            empty_w(4, 1, "s")
-            turn_w(5, 1)
-            mix(2)
-            turn_w(7, 0)
-            empty_w(5, 1, "s")
-            mix(3)
-            gelu(1)
+            gelu(3)
             quant_w(4)
-            turn_w(5, 0)
-            pair(1)
-            diag_z(4, "s")
-            pair(0)
-            empty_f0(1, 0, "s")
-            empty_w(7, 0, "s")
-            widen(6, 0)
-            mul_m(4)
-            widen(6, 1)
-            turn_f1(1)
-            quant_w(7)
-            mix(0)
-            turn_w(6, 0)
-            turn_w(6, 1)
-            mul_m(7)
-            weights()
-            empty_w(5, 0, "s")
-            quant_w(5)
-            gelu(4)
-            mul_m(5)
-            empty_w(6, 1, "s")
+            mix(2)
+            empty_f0(1)
+            turn_w(5)
+            widen(7)
             mix(1)
-            empty_w(6, 0, "s")
-            quant_f0(3)
+            turn_w(6)
+            mul_m(4)
+            empty_w(5)
+            empty_w(6)
+            pair(0)
+            turn_w(7)
             quant_w(6)
-            gelu(7)
-            weave_y(0, 2, "s")
+            gelu(0)
             quant_f0(2)
-            weave_y(0, 1, "s")
-            quant_f1(3)
-            pair(4)
-            pair(7)
-            mix(4)
-            weave_y(0, 3, "s")
-            gelu(5)
-            mix(7)
+            empty_w(7)
+            diag_z(4, "s")
+            mix(0)
+            weights()
+            pair(3)
             mul_m(6)
-            pair(5)
-            quant_f0(0)
-            gelu(6)
-            load_f1(2)
-            mix(5)
-            weave_y(0, 0, "s")
-            pair(6)
-            mix(6)
-            weave_y(1, 3, "v")
-            turn_f1(2)
-            mul_h0(0)
-            weave_y(1, 0, "v")
-            weave_y(1, 1, "s")
-            mul_h0(3)
-            quant_y(0)
-            weave_y(1, 2, "s")
-            quant_y(1)
-            quant_f0(1)
+            gelu(4)
             quant_f1(0)
-            keep_h0(0)
-            keep_h0(3)
-            mul_h1(3)
-            empty_f1(2, "s")
-            empty_f1(1, "s")
-            blend(3)
-            mul_h0(2)
-            quant_f1(2)
-            mul_h0(1)
-            keep_h0(2)
+            mix(3)
+            quant_w(7)
+            gelu(6)
+            pair(4)
+            quant_w(5)
+            diag_z(7, "s")
+            weave_y(0, 2, "s")
+            weave_y(0, 0, "s")
             quant_f1(1)
+            pair(6)
+            mul_m(7)
+            gelu(7)
+            mix(6)
+            mul_m(5)
+            mix(4)
+            weave_y(0, 1, "s")
+            quant_f0(1)
+            quant_f0(0)
+            pair(7)
+            mix(7)
+            gelu(5)
+            weave_y(0, 3, "s")
+            pair(5)
+            mix(5)
+            turn_f1(2)
+            quant_y(0)
+            weave_y(1, 1, "s")
+            turn_f1(3)
+            mul_h0(0)
+            weave_y(1, 0, "s")
+            weave_y(1, 3, "v")
+            mul_h0(1)
+            keep_h0(0)
             keep_h0(1)
+            weave_y(1, 2, "v")
+            quant_y(1)
+            quant_f0(3)
             mul_h1(0)
-            mul_h1(1)
             blend(0)
-            blend(1, 2)
+            mul_h1(1)
+            blend(1)
+            empty_f1(3)
+            mul_h0(2)
+            empty_f1(2)
+            quant_f1(3)
+            keep_h0(2)
+            mul_h0(3)
+            quant_f1(2)
             mul_h1(2)
             blend(2)
+            keep_h0(3)
+            mul_h1(3)
+            blend(3, 2)

from contextlib import ExitStack

import concourse.mybir as mybir
from concourse.masks import make_identity

F32 = mybir.dt.float32
BF16 = mybir.dt.bfloat16
U32 = mybir.dt.uint32
U8 = mybir.dt.uint8
FP8 = mybir.dt.float8_e4m3fn
FP8X4 = mybir.dt.float8_e4m3fn_x4
ACT = mybir.ActivationFunctionType
ALU = mybir.AluOpType

P = 128
PACK = 4
K_PASS = P * PACK
BATCH, FINE, FEATURES, HORIZON = 2, 2048, 256, 512
COARSE = FINE // 2
COLS = BATCH * FEATURES
FINE_PASSES = FINE // K_PASS
COARSE_PASSES = COARSE // K_PASS
MIX_TILES = COARSE // P
OUT_TILES = HORIZON // P

PE_GAIN_PASS = 3
PASS_ORDER = (0, 3, 1, 2)
FLOPS = 2 * COLS * (COARSE * FINE + HORIZON * FINE + HORIZON * COARSE)


def tile_timemixerpyramidforecast_kernel(tc, x, g0, w01_bytes, w01_scale, g1, f0, f1, ens, out):
    nc = tc.nc
    with ExitStack() as ctx:
        keep = ctx.enter_context(tc.tile_pool(name="keep", bufs=1))
        work = ctx.enter_context(tc.tile_pool(name="work", bufs=2))
        psum = ctx.enter_context(tc.psum_pool(name="psum", bufs=2))

        def kept(name, shape, dtype):
            return keep.tile(shape, dtype, name=name, align_bytes=64)

        scale_rows = kept("scale_rows", [P, P], F32)
        scale_cols = kept("scale_cols", [P, 16], F32)
        scale = kept("scale", [P, FINE], F32)
        g0_col = kept("g0_col", [P, FINE_PASSES, 16], BF16)
        g1_col = kept("g1_col", [P, COARSE_PASSES, PACK], BF16)
        g1_half = kept("g1_half", [P, COARSE_PASSES, PACK], F32)
        ens_col = kept("ens_col", [P, OUT_TILES], BF16)
        tanh_col = kept("tanh_col", [P, OUT_TILES], F32)
        a_col = kept("a_col", [P, OUT_TILES], F32)
        rest_col = kept("rest_col", [P, OUT_TILES], F32)
        zero = kept("zero", [P, 1], F32)
        table_out = kept("table_out", [P, 1], F32)
        ident = kept("ident", [P, P], F32)
        ident_bf = kept("ident_bf", [P, P], BF16)
        gain_diag = kept("gain_diag", [P, PACK, P], BF16)
        pair_diag = [kept(f"pair_diag{j}", [P, P], BF16) for j in range(MIX_TILES)]

        w_raw = [kept(f"w_raw{j}", [P, FINE], U8) for j in range(MIX_TILES)]
        x_fine = [kept(f"x_fine{g}", [P, BATCH, PACK * FEATURES], BF16) for g in range(FINE_PASSES)]
        x_pair = [kept(f"x_pair{g}", [P, BATCH, 2 * PACK * FEATURES], BF16) for g in range(COARSE_PASSES)]
        f0_raw = [kept(f"f0_raw{i}", [P, FINE], BF16) for i in range(OUT_TILES)]
        f1_raw = [kept(f"f1_raw{i}", [P, COARSE], BF16) for i in range(OUT_TILES)]

        def operand(name, words):
            return kept(name + "_codes", [P, words], U32), kept(name + "_scales", [P, words], U8)

        u_mx = [operand(f"u{g}", COLS) for g in range(FINE_PASSES)]
        y_mx = [operand(f"y{g}", COLS) for g in range(COARSE_PASSES)]
        w_mx = [operand(f"w{j}", FINE // PACK) for j in range(MIX_TILES)]
        f0_mx = [operand(f"f0_{i}", FINE // PACK) for i in range(OUT_TILES)]
        f1_mx = [operand(f"f1_{i}", COARSE // PACK) for i in range(OUT_TILES)]
        y_planes = [kept(f"y_planes{g}", [P, PACK, COLS], BF16) for g in range(COARSE_PASSES)]
        h0_part = [kept(f"h0_part{i}", [P, COLS], F32) for i in range(OUT_TILES)]

        live = {}
        depth = {"w_bf": 3, "w_g": 3, "f0_g": 4, "f1_g": 2, "x_s": 2, "u_g": 2, "gelu": 3, "y_g": 2, "o": 3, "tp": 4, "m": 2, "acc": 2}

        def made(tag, n, shape, dtype):
            if (tag, n) not in live:
                live[tag, n] = work.tile(shape, dtype, name=tag, bufs=depth[tag], align_bytes=64)
            return live[tag, n]

        def bank(tag, key, shape):
            live[key] = psum.tile(shape, F32, name=tag, bufs=depth[tag])
            return live[key]

        w_rows = w01_bytes.rearrange("(g m t) k -> g t m k", g=COARSE_PASSES, t=PACK)
        f0_rows = f0.rearrange("(m t) k -> t m k", t=PACK)
        f1_rows = f1.rearrange("(m t) k -> t m k", t=PACK)
        out_rows = out.rearrange("b (m t) n -> t m b n", t=PACK)

        def load_scales():
            nc.sync.dma_start(out=scale_rows[0:16, :], in_=w01_scale.rearrange("o (r n) -> (o r) n", n=P))

        def load_g0(g):
            nc.sync.dma_start(out=g0_col[:, g, 0:PACK], in_=g0[g * K_PASS : (g + 1) * K_PASS].rearrange("(p t) -> p t", t=PACK))

        def load_g1_ens():
            nc.sync.dma_start(out=g1_col[:], in_=g1.rearrange("(g p t) -> p g t", p=P, t=PACK))
            nc.sync.dma_start(out=ens_col[:], in_=ens.rearrange("(m t) -> m t", t=PACK))

        def load_w(j):
            nc.sync.dma_start(out=w_raw[j][:], in_=w_rows[j // PACK, j % PACK])

        def load_x(g):
            for b in range(BATCH):
                nc.sync.dma_start(out=x_fine[g][:, b, :], in_=x[b, g * K_PASS : (g + 1) * K_PASS, :].rearrange("(p t) n -> p (t n)", t=PACK))

        def load_pair(g):
            steps = slice(2 * g * K_PASS, 2 * (g + 1) * K_PASS)
            nc.sync.dma_start(out=x_pair[g][:], in_=x[:, steps, :].rearrange("b (p s) n -> p b (s n)", s=2 * PACK))

        def load_f0(i):
            nc.sync.dma_start(out=f0_raw[i][:], in_=f0_rows[i])

        def load_f1(i):
            nc.sync.dma_start(out=f1_raw[i][:], in_=f1_rows[i])

        def turn_scales():
            nc.tensor.transpose(bank("tp", ("scales", 0), [P, P])[:], scale_rows[:], ident[:])

        def fetch_scales():
            nc.scalar.copy(out=scale_cols[:], in_=live["scales", 0][:, 0:16])

        def spread(q):
            spot = bank("tp", ("spread", q), [P, 4, P])
            for i in range(4):
                r = 4 * q + i
                nc.tensor.transpose(spot[:, i, :], scale_cols[:, r : r + 1].to_broadcast([P, P]), ident[:])

        def spread_out(q, eng):
            copy_of(eng)(out=scale[:, q * 512 : (q + 1) * 512], in_=live["spread", q][:].rearrange("p r n -> p (r n)"))

        def copy_of(eng):
            return nc.scalar.copy if eng == "s" else nc.vector.tensor_copy

        def turn(src, half, key):
            words = src[:].bitcast(F32)
            spot = bank("tp", key, [P, 2, 2, P])
            for g in range(2):
                lo = (2 * half + g) * K_PASS // 2
                for e in range(2):
                    nc.tensor.transpose(spot[:, g, e, :], words[:, lo + e : lo + K_PASS // 2 : 2], ident[:])

        def empty(dst, half, key):
            n = 2 * K_PASS
            nc.scalar.copy(
                out=dst[:, half * n : (half + 1) * n].bitcast(F32).rearrange("p (g r e) -> p g r e", g=2, e=2),
                in_=live[key][:].rearrange("p g e r -> p g r e"),
            )

        def quantise(operand_tiles, src):
            codes, scales = operand_tiles
            nc.vector.quantize_mx(out=codes[:].bitcast(FP8X4), scales=scales[:], in_=src[:])

        def widen(j, chunks=1):
            dst = made("w_bf", j, [P, FINE], BF16)
            n = FINE // chunks
            for c in range(chunks):
                cols = slice(c * n, (c + 1) * n)
                nc.vector.tensor_tensor(out=dst[:, cols], in0=w_raw[j][:, cols].bitcast(FP8), in1=scale[:, cols], op=ALU.mult)

        def turn_w(j):
            for half in range(2):
                turn(live["w_bf", j], half, ("w_turned", j, half))

        def empty_w(j):
            for half in range(2):
                empty(made("w_g", j, [P, FINE], BF16), half, ("w_turned", j, half))

        def quant_w(j):
            quantise(w_mx[j], live["w_g", j])

        def turn_f0(i):
            for half in range(2):
                turn(f0_raw[i], half, ("f0_turned", i, half))

        def empty_f0(i):
            for half in range(2):
                empty(made("f0_g", i, [P, FINE], BF16), half, ("f0_turned", i, half))

        def quant_f0(i):
            quantise(f0_mx[i], live["f0_g", i])

        def turn_f1(i):
            turn(f1_raw[i], 0, ("f1_turned", i))

        def empty_f1(i):
            empty(made("f1_g", i, [P, COARSE], BF16), 0, ("f1_turned", i))

        def quant_f1(i):
            quantise(f1_mx[i], live["f1_g", i])

        def gain(g):
            dst = made("x_s", g, [P, PACK, COLS], BF16)
            for t in range(PACK):
                nc.vector.tensor_scalar(
                    out=dst[:, t, :].rearrange("p (b n) -> p b n", b=BATCH),
                    in0=x_fine[g][:, :, t * FEATURES : (t + 1) * FEATURES],
                    scalar1=g0_col[:, g, t : t + 1],
                    scalar2=None,
                    op0=ALU.mult,
                )

        def weave(dst, src, c0, c1, eng):
            copy_of(eng)(
                out=dst[:, PACK * c0 : PACK * c1].rearrange("p (c i t) -> p c t i", i=4, t=PACK),
                in_=src[:, :, c0:c1].rearrange("p t (c i) -> p c t i", i=4),
            )

        def weave_u(g, b, eng):
            weave(made("u_g", g, [P, PACK * COLS], BF16), live["x_s", g], b * FEATURES, (b + 1) * FEATURES, eng)

        def make_gain_diag():
            for t in range(PACK):
                nc.vector.tensor_scalar(out=gain_diag[:, t, :], in0=ident_bf[:], scalar1=g0_col[:, PE_GAIN_PASS, t : t + 1], scalar2=None, op0=ALU.mult)

        def gain_mm(q):
            g, b, n0 = PE_GAIN_PASS, q // 2, (q % 2) * P
            spot = bank("acc", ("gained", q), [P, PACK, P])
            for t in range(PACK):
                lo = t * FEATURES + n0
                nc.tensor.matmul(spot[:, t, :], lhsT=gain_diag[:, t, :], rhs=x_fine[g][:, b, lo : lo + P], start=True, stop=True)

        def gain_out(q):
            nc.scalar.copy(
                out=made("u_g", PE_GAIN_PASS, [P, PACK * COLS], BF16)[:, q * K_PASS : (q + 1) * K_PASS].rearrange("p (n t) -> p n t", t=PACK),
                in_=live["gained", q][:].rearrange("p t n -> p n t"),
            )

        def quant_u(g):
            quantise(u_mx[g], live["u_g", g])

        def multiply(tag, key, stationary, moving, passes):
            acc = bank(tag, key, [P, COLS])
            codes, scales = stationary
            for g in passes:
                rows = slice(g * P, (g + 1) * P)
                nc.tensor.matmul_mx(
                    out=acc[:],
                    lhsT=codes[:, rows].bitcast(FP8X4),
                    lhsT_scale=scales[:, rows],
                    rhs=moving[g][0][:].bitcast(FP8X4),
                    rhs_scale=moving[g][1][:],
                    start=(g == passes[0]),
                    stop=(g == passes[-1]),
                )

        def mul_m(j):
            multiply("m", ("m", j), w_mx[j], u_mx, PASS_ORDER)

        def mul_h0(i):
            multiply("acc", ("h0", i), f0_mx[i], u_mx, PASS_ORDER)

        def mul_h1(i):
            multiply(("acc", "m", "m", "acc")[i], ("h1", i), f1_mx[i], y_mx, (0, 1))

        def halve_gains():
            nc.gpsimd.tensor_scalar(out=g1_half[:], in0=g1_col[:], scalar1=0.5, scalar2=0.0, op0=ALU.mult, op1=ALU.add)

        def diag_z(j, eng):
            col = g1_half[:, j // PACK, j % PACK : j % PACK + 1]
            if eng == "s":
                nc.scalar.activation(out=pair_diag[j][:], in_=ident_bf[:], func=ACT.Copy, scale=col)
            else:
                nc.vector.tensor_scalar(out=pair_diag[j][:], in0=ident_bf[:], scalar1=col, scalar2=None, op0=ALU.mult)

        def pair(j):
            acc = bank("acc", ("z", j), [P, COLS])
            for e in range(2):
                s = 2 * (j % PACK) + e
                nc.tensor.matmul(
                    acc[:].rearrange("p (b n) -> p b n", b=BATCH),
                    lhsT=pair_diag[j][:],
                    rhs=x_pair[j // PACK][:, :, s * FEATURES : (s + 1) * FEATURES],
                    start=(e == 0),
                    stop=(e == 1),
                )

        def gelu(j):
            nc.scalar.activation(out=made("gelu", j, [P, COLS], F32)[:], in_=live["m", j][:], func=ACT.Gelu_apprx_tanh)

        def mix(j):
            g, t = j // PACK, j % PACK
            nc.vector.scalar_tensor_tensor(
                out=y_planes[g][:, t, :], in0=live["gelu", j][:], scalar=g1_col[:, g, t : t + 1], in1=live["z", j][:], op0=ALU.mult, op1=ALU.add
            )

        def weave_y(g, q, eng):
            weave(made("y_g", g, [P, PACK * COLS], BF16), y_planes[g], q * P, (q + 1) * P, eng)

        def quant_y(g):
            quantise(y_mx[g], live["y_g", g])

        def weights():
            nc.scalar.activation(out=tanh_col[:], in_=ens_col[:], func=ACT.Tanh, scale=0.5)
            nc.gpsimd.tensor_scalar(out=a_col[:], in0=tanh_col[:], scalar1=0.5, scalar2=0.5, op0=ALU.mult, op1=ALU.add)
            nc.gpsimd.tensor_scalar(out=rest_col[:], in0=tanh_col[:], scalar1=-0.5, scalar2=0.5, op0=ALU.mult, op1=ALU.add)

        def keep_h0(i):
            nc.scalar.activation(out=h0_part[i][:], in_=live["h0", i][:], func=ACT.Copy, scale=a_col[:, i : i + 1])

        def blend(i, pieces=1):
            o = made("o", i, [P, COLS], F32)
            n = BATCH // pieces
            for c in range(pieces):
                cols = slice(c * n * FEATURES, (c + 1) * n * FEATURES)
                nc.vector.scalar_tensor_tensor(
                    out=o[:, cols], in0=live["h1", i][:, cols], scalar=rest_col[:, i : i + 1], in1=h0_part[i][:, cols], op0=ALU.mult, op1=ALU.add
                )
                nc.sync.dma_start(out=out_rows[i][:, c * n : (c + 1) * n, :], in_=o[:, cols].rearrange("p (b n) -> p b n", n=FEATURES))

        nc.gpsimd.memset(scale_rows[:], 0.0)
        make_identity(nc, ident[:])
        nc.gpsimd.tensor_copy(out=ident_bf[:], in_=ident[:])
        nc.vector.memset(zero[:], 0.0)
        nc.scalar.activation(out=table_out[:], in_=zero[:], func=ACT.Gelu_apprx_tanh)

        with tc.manual_schedule():
            load_scales()
            load_x(0)
            load_g0(0)
            load_g0(3)
            load_w(0)
            load_f0(2)
            load_w(1)
            load_x(3)
            load_w(3)
            load_w(2)
            load_g0(1)
            load_x(1)
            load_f1(1)
            load_f0(3)
            load_g1_ens()
            load_f1(0)
            load_x(2)
            load_w(4)
            load_f0(0)
            load_pair(0)
            load_g0(2)
            load_f0(1)
            load_w(7)
            load_w(5)
            load_w(6)
            load_f1(3)
            load_pair(1)
            load_f1(2)
            turn_scales()
            fetch_scales()
            spread(0)
            gain(0)
            spread(1)
            make_gain_diag()
            spread_out(0, "s")
            spread(2)
            spread(3)
            spread_out(1, "s")
            spread_out(2, "s")
            spread_out(3, "s")
            widen(0, 4)
            widen(1)
            turn_w(0)
            widen(2)
            weave_u(0, 1, "s")
            gain(1)
            turn_f0(2)
            gain_mm(2)
            empty_w(0)
            weave_u(0, 0, "s")
            widen(3)
            quant_w(0)
            gain_mm(0)
            empty_f0(2)
            turn_w(1)
            empty_w(1)
            turn_f1(1)
            empty_f1(1)
            halve_gains()
            gain_out(0)
            diag_z(1, "v")
            turn_w(2)
            empty_w(2)
            turn_f0(3)
            diag_z(2, "v")
            empty_f0(3)
            gain_out(2)
            quant_w(1)
            turn_w(3)
            turn_f1(0)
            gain_mm(3)
            empty_w(3)
            quant_u(0)
            gain_mm(1)
            empty_f1(0)
            widen(4)
            weave_u(1, 1, "v")
            turn_f0(0)
            quant_w(2)
            gain_out(1)
            gain_out(3)
            quant_u(3)
            weave_u(1, 0, "s")
            turn_w(4)
            empty_f0(0)
            gain(2)
            weave_u(2, 0, "s")
            quant_u(1)
            weave_u(2, 1, "v")
            pair(2)
            quant_w(3)
            diag_z(6, "s")
            empty_w(4)
            pair(1)
            diag_z(3, "s")
            diag_z(5, "s")
            quant_u(2)
            turn_f0(1)
            mul_m(1)
            gelu(1)
            mul_m(2)
            widen(5)
            widen(6)
            diag_z(0, "s")
            mul_m(3)
            gelu(2)
            mul_m(0)
            gelu(3)
            quant_w(4)
            mix(2)
            empty_f0(1)
            turn_w(5)
            widen(7)
            mix(1)
            turn_w(6)
            mul_m(4)
            empty_w(5)
            empty_w(6)
            pair(0)
            turn_w(7)
            quant_w(6)
            gelu(0)
            quant_f0(2)
            empty_w(7)
            diag_z(4, "s")
            mix(0)
            weights()
            pair(3)
            mul_m(6)
            gelu(4)
            quant_f1(0)
            mix(3)
            quant_w(7)
            gelu(6)
            pair(4)
            quant_w(5)
            diag_z(7, "s")
            weave_y(0, 2, "s")
            weave_y(0, 0, "s")
            quant_f1(1)
            pair(6)
            mul_m(7)
            gelu(7)
            mix(6)
            mul_m(5)
            mix(4)
            weave_y(0, 1, "s")
            quant_f0(1)
            quant_f0(0)
            pair(7)
            mix(7)
            gelu(5)
            weave_y(0, 3, "s")
            pair(5)
            mix(5)
            turn_f1(2)
            quant_y(0)
            weave_y(1, 1, "s")
            turn_f1(3)
            mul_h0(0)
            weave_y(1, 0, "s")
            weave_y(1, 3, "v")
            mul_h0(1)
            keep_h0(0)
            keep_h0(1)
            weave_y(1, 2, "v")
            quant_y(1)
            quant_f0(3)
            mul_h1(0)
            blend(0)
            mul_h1(1)
            blend(1)
            empty_f1(3)
            mul_h0(2)
            empty_f1(2)
            quant_f1(3)
            keep_h0(2)
            mul_h0(3)
            quant_f1(2)
            mul_h1(2)
            blend(2)
            keep_h0(3)
            mul_h1(3)
            blend(3, 2)
